import numpy as np
import ml_dtypes


def mxq(x, axis, fmt="e4m3"):
    dtype, down = {"e4m3": (ml_dtypes.float8_e4m3fn, 7), "e5m2": (ml_dtypes.float8_e5m2, 14)}[fmt]
    v = np.moveaxis(np.asarray(x, np.float32).astype(ml_dtypes.bfloat16).astype(np.float64), axis, -1)
    blocks = v.reshape(v.shape[:-1] + (-1, 32))
    amax = np.abs(blocks).max(-1, keepdims=True)
    byte = np.maximum(np.where(amax > 0, np.frexp(amax)[1] - 1 + 127, 0) - down, 1)
    scale = np.exp2(byte - 127.0)
    codes = (blocks / scale).astype(np.float32).astype(dtype).astype(np.float64)
    return np.moveaxis((codes * scale).reshape(v.shape), -1, axis)


WIDE = False


def mx_kscale(k):
    if not WIDE:
        return np.ones(k)
    levels = np.array([10, -10, 5, -5, 0])
    if k % 512:
        return np.exp2(np.random.permutation(np.resize(levels, k // 32))).repeat(32)
    a = np.empty((k // 512, 16))
    for p in range(k // 512):
        a[p, :8] = np.random.permutation(np.resize(levels, 8))
        for g in range(8):
            far = levels[np.abs(levels - a[p, g]) >= 10]
            a[p, g + 8] = far[np.random.randint(len(far))]
    return np.exp2(a.ravel()).repeat(32)


def f64(x):
    return np.asarray(x).astype(np.float64)


def striped(idx):
    return np.tile(idx.reshape(-1, 16).T, (8, 1)).astype(np.uint16)


def unstriped(offs):
    return offs[:16].T.reshape(-1).astype(np.int64)


def pack_weight(w):
    k, n = w.shape
    w = f64(np.asarray(w, np.float32).astype(ml_dtypes.bfloat16)).reshape(k // 32, 32, n)
    amax = np.abs(w).max(1)
    byte = np.clip(np.where(amax > 0, np.frexp(amax)[1] - 1 + 127 - 7, 1), 1, 254)
    scaled = (w * np.exp2(127.0 - byte)[:, None, :]).reshape(k, n).astype(np.float32)
    words = np.ascontiguousarray(scaled.reshape(k // 512, 128, 4, n).transpose(0, 1, 3, 2)).astype(ml_dtypes.float8_e4m3fn).view(np.uint8)
    return words, np.ascontiguousarray(byte.astype(np.uint8).reshape(k // 512, 16, n))


def unpack_weight(words, scales):
    g, p, n, _ = words.shape
    vals = np.ascontiguousarray(words).view(ml_dtypes.float8_e4m3fn).astype(np.float64) * np.repeat(np.exp2(scales.astype(np.float64) - 127.0), 8, axis=1)[..., None]
    return vals.transpose(0, 1, 3, 2).reshape(g * 512, n)


def planes(y):
    n, m = y.shape
    v = y.astype(np.float32).astype(ml_dtypes.bfloat16).astype(np.float64).reshape(n // 32, 32, m)
    top = np.abs(v).max(1)
    byte = np.clip(np.where(top > 0, np.frexp(top)[1] - 1 + 127 - 7, 1), 1, 254)
    codes = (v * np.exp2(127.0 - byte)[:, None, :]).reshape(n, m).astype(np.float32).astype(ml_dtypes.float8_e4m3fn).view(np.uint8)
    words = codes.reshape(n // 512, 128, 4, m).transpose(0, 1, 3, 2)
    return np.ascontiguousarray(words), np.ascontiguousarray(byte.astype(np.uint8).reshape(n // 512, 16, m))


def gelu(v):
    return 0.5 * v * (1.0 + np.tanh(np.sqrt(2.0 / np.pi) * (v + 0.044715 * v**3)))


K, T, S, W, H, N = 512, 2048, 512, 1024, 512, 512


def setup_inputs():
    n = np.random.standard_normal
    s = mx_kscale(K)[:, None]
    u = mx_kscale(H)
    packed_xT = pack_weight(n((K, T)) * s)
    packed_eT = pack_weight(n((K, W)) * s)
    packed_yT = pack_weight(n((K, W)) * s)
    return {
        "x_words": packed_xT[0],
        "x_scales": packed_xT[1],
        "e_words": packed_eT[0],
        "e_scales": packed_eT[1],
        "y_words": packed_yT[0],
        "y_scales": packed_yT[1],
        "w1": (n((K, H)) / np.sqrt(3 * K) / s * u).astype(np.float32),
        "w2": (n((K, H)) / np.sqrt(3 * K) / s * u).astype(np.float32),
        "w3": (n((K, H)) / np.sqrt(3 * K) / s * u).astype(np.float32),
        "w4": (n((H, N)) / np.sqrt(H) / u[:, None]).astype(np.float32),
        "offs": striped(np.random.permutation(T)[:S]),
        "tok": striped(np.random.permutation(W)[:S]),
        "row": striped(np.random.permutation(W)[:S]),
    }


def reference(x_words, x_scales, e_words, e_scales, y_words, y_scales, w1, w2, w3, w4, offs, tok, row):
    xq = unpack_weight(x_words, x_scales)[:, unstriped(offs)]
    e_tok = unpack_weight(e_words, e_scales)[:, unstriped(tok)]
    y_row = unpack_weight(y_words, y_scales)[:, unstriped(row)]
    h = gelu(mxq(f64(w1), 0, "e4m3").T @ xq + mxq(f64(w2), 0, "e4m3").T @ e_tok + mxq(f64(w3), 0, "e4m3").T @ y_row)
    out_0 = mxq(f64(w4), 0, "e4m3").T @ mxq(h, 0, "e4m3")
    return (out_0,) + planes(out_0)

@@ -1,0 +1,192 @@
+from contextlib import ExitStack
+
+import concourse.mybir as mybir
+
+F32 = mybir.dt.float32
+BF16 = mybir.dt.bfloat16
+I32 = mybir.dt.int32
+U32 = mybir.dt.uint32
+U16 = mybir.dt.uint16
+U8 = mybir.dt.uint8
+FP8X4 = mybir.dt.float8_e4m3fn_x4
+GELU = mybir.ActivationFunctionType.Gelu_apprx_tanh
+
+P = 128
+PACK = 4
+WIDTH = 512
+TOKENS = 512
+CHUNK = 128
+CHUNKS = TOKENS // CHUNK
+FLOPS = 4 * 2 * 512 * 512 * 512
+
+
+def tile_picked_zlayout_gelu_po_kernel(
+    tc, x_words, x_scales, e_words, e_scales, y_words, y_scales, w1, w2, w3, w4, offs, tok, row, out_0, out_1, out_2
+):
+    nc = tc.nc
+    with ExitStack() as ctx:
+        keep = ctx.enter_context(tc.tile_pool(name="keep", bufs=1))
+        psum = ctx.enter_context(tc.psum_pool(name="psum", bufs=1))
+
+        def sb(name, shape, dtype):
+            return keep.tile(shape, dtype, name=name, align_bytes=64)
+
+        names = ("x", "e", "y")
+        words_in = (x_words, e_words, y_words)
+        scales_in = (x_scales, e_scales, y_scales)
+        lists_in = (offs, tok, row)
+        first_row = (0, 4, 8)
+        columns = [w.shape[2] for w in words_in]
+
+        lists = [sb("list_" + n, [P, TOKENS // 16], U16) for n in names]
+        table_words = [sb("words_" + n, [P, columns[i]], I32) for i, n in enumerate(names)]
+        table_scales = [sb("scales_" + n, [P, columns[i]], U8) for i, n in enumerate(names)]
+        raw = [sb("raw_%d" % i, [P, PACK, WIDTH], F32) for i in range(3)]
+        raw4 = [sb("raw4_%d" % i, [P, PACK, WIDTH // 2], F32) for i in range(2)]
+        warm_in = sb("warm_in", [P, 8], F32)
+        warm_out = sb("warm_out", [P, 8], F32)
+
+        for i in range(3):
+            nc.vector.memset(table_scales[i][:].bitcast(I32), 0)
+        nc.gpsimd.memset(warm_in[:], 0.0)
+
+        def load_weight(dst, w, c0, c1):
+            nc.sync.dma_start(out=dst[:], in_=w.rearrange("(p j) c -> p j c", j=PACK)[:, :, c0:c1])
+
+        def load_words(i):
+            nc.sync.dma_start(out=table_words[i][:], in_=words_in[i][0].rearrange("p n t -> p (n t)").bitcast(I32))
+
+        def load_scales(i):
+            for q in range(4):
+                p0 = 32 * q + first_row[i]
+                nc.scalar.dma_start(
+                    out=table_scales[i][p0 : p0 + 4, :].bitcast(I32),
+                    in_=scales_in[i][0, 4 * q : 4 * q + 4, :].bitcast(I32),
+                )
+
+        load_weight(raw[0], w1, 0, WIDTH)
+        nc.sync.dma_start(lists[0][:], offs)
+        load_scales(0)
+        load_weight(raw[1], w2, 0, WIDTH)
+        nc.sync.dma_start(lists[1][:], tok)
+        nc.sync.dma_start(lists[2][:], row)
+        load_scales(1)
+        load_scales(2)
+        nc.scalar.activation(warm_out[:], warm_in[:], GELU)
+        load_weight(raw[2], w3, 0, WIDTH)
+        for i in range(3):
+            load_words(i)
+        load_weight(raw4[0], w4, 0, WIDTH // 2)
+        load_weight(raw4[1], w4, WIDTH // 2, WIDTH)
+
+        picked_scales = [sb("picked_scales_" + n, [P, TOKENS], U8) for n in names]
+        for i in range(3):
+            nc.vector.tensor_copy(picked_scales[i][:], table_scales[i][:].indirect(lists[i][:]))
+
+        grouped = [sb("grouped_%d" % i, [P, PACK, P, PACK], BF16) for i in range(4)]
+        w_codes = [sb("w_codes_%d" % i, [P, WIDTH], U32) for i in range(4)]
+        w_scales = [sb("w_scales_%d" % i, [P, WIDTH], U8) for i in range(4)]
+
+        def deal(copy, i, src, m0, m1):
+            copy(
+                out=grouped[i][:, :, m0:m1, :].rearrange("p t m j -> p m j t"),
+                in_=src.rearrange("p j (m t) -> p m j t", t=PACK),
+            )
+
+        def quantize_weight(i):
+            nc.vector.quantize_mx(
+                out=w_codes[i][:].bitcast(FP8X4),
+                scales=w_scales[i][:],
+                in_=grouped[i][:].rearrange("p t m j -> p (t m j)"),
+            )
+
+        for i in range(3):
+            deal(nc.scalar.copy, i, raw[i][:], 0, P)
+            quantize_weight(i)
+
+        picked = [sb("picked_" + n, [P, TOKENS], U32) for n in names[:2]]
+        for i in range(2):
+            nc.vector.tensor_copy(picked[i][:], table_words[i][:].bitcast(U32).indirect(lists[i][:]))
+        picked_y = [sb("picked_y_%d" % c, [P, CHUNK], U32) for c in range(CHUNKS)]
+        for c in range(CHUNKS):
+            nc.vector.tensor_copy(
+                picked_y[c][:], table_words[2][:].bitcast(U32).indirect(lists[2][:, c * CHUNK // 16 : (c + 1) * CHUNK // 16])
+            )
+
+        hidden = [psum.tile([P, PACK, CHUNK], F32, name="hidden_%d" % c) for c in range(CHUNKS)]
+        result = [psum.tile([P, PACK, CHUNK], F32, name="result_%d" % c) for c in range(CHUNKS)]
+
+        def first_layer_pass(i, c, t):
+            cols = slice(c * CHUNK, (c + 1) * CHUNK)
+            slot = slice(t * P, (t + 1) * P)
+            codes = picked_y[c][:] if i == 2 else picked[i][:, cols]
+            nc.tensor.matmul_mx(
+                out=hidden[c][:, t, :],
+                lhsT=w_codes[i][:, slot].bitcast(FP8X4),
+                lhsT_scale=w_scales[i][:, slot],
+                rhs=codes.bitcast(FP8X4),
+                rhs_scale=picked_scales[i][first_row[i] : P, cols],
+                start=(i == 0),
+                stop=(i == 2),
+            )
+
+        for i in range(2):
+            for c in range(CHUNKS):
+                first_layer_pass(i, c, 0)
+
+        h_bf = [sb("h_bf_%d" % c, [P, CHUNK, PACK], BF16) for c in range(CHUNKS)]
+        h_codes = [sb("h_codes_%d" % c, [P, CHUNK], U32) for c in range(CHUNKS)]
+        h_scales = [sb("h_scales_%d" % c, [P, CHUNK], U8) for c in range(CHUNKS)]
+        for c in range(CHUNKS):
+            first_layer_pass(2, c, 0)
+            for t in range(1, PACK):
+                for i in range(3):
+                    first_layer_pass(i, c, t)
+            nc.scalar.activation(h_bf[c][:], hidden[c][:].rearrange("p t n -> p n t"), GELU)
+
+        deal(nc.vector.tensor_copy, 3, raw4[0][:], 0, P // 2)
+        deal(nc.vector.tensor_copy, 3, raw4[1][:], P // 2, P)
+        quantize_weight(3)
+        for c in range(CHUNKS):
+            nc.vector.quantize_mx(
+                out=h_codes[c][:].bitcast(FP8X4), scales=h_scales[c][:], in_=h_bf[c][:].rearrange("p n t -> p (n t)")
+            )
+
+        out_f32 = [sb("out_f32_%d" % c, [P, PACK, CHUNK], F32) for c in range(CHUNKS)]
+        out_bf = [sb("out_bf_%d" % c, [P, CHUNK, PACK], BF16) for c in range(CHUNKS)]
+        out_codes = sb("out_codes", [P, TOKENS], U32)
+        out_scales = sb("out_scales", [P, TOKENS], U8)
+        out_rows = out_0.rearrange("(p t) n -> p t n", t=PACK)
+        out_words = out_1[0].rearrange("p n t -> p (n t)").bitcast(I32)
+        for c in range(CHUNKS):
+            cols = slice(c * CHUNK, (c + 1) * CHUNK)
+            for t in range(PACK):
+                slot = slice(t * P, (t + 1) * P)
+                nc.tensor.matmul_mx(
+                    out=result[c][:, t, :],
+                    lhsT=w_codes[3][:, slot].bitcast(FP8X4),
+                    lhsT_scale=w_scales[3][:, slot],
+                    rhs=h_codes[c][:].bitcast(FP8X4),
+                    rhs_scale=h_scales[c][:],
+                    start=True,
+                    stop=True,
+                )
+            nc.scalar.copy(out=out_f32[c][:], in_=result[c][:])
+            nc.sync.dma_start(out=out_rows[:, :, cols], in_=out_f32[c][:])
+            nc.vector.tensor_copy(
+                out=out_bf[c][:].rearrange("p (a b) t -> p a t b", b=4),
+                in_=out_f32[c][:].rearrange("p t (a b) -> p a t b", b=4),
+            )
+            nc.vector.quantize_mx(
+                out=out_codes[:, cols].bitcast(FP8X4),
+                scales=out_scales[:, cols],
+                in_=out_bf[c][:].rearrange("p n t -> p (n t)"),
+            )
+            if c % 2 == 1:
+                pair = slice((c - 1) * CHUNK, (c + 1) * CHUNK)
+                nc.sync.dma_start(out=out_words[:, pair], in_=out_codes[:, pair].bitcast(I32))
+        for q in range(4):
+            queue = nc.scalar if q % 2 else nc.sync
+            queue.dma_start(
+                out=out_2[0, 4 * q : 4 * q + 4, :].bitcast(I32), in_=out_scales[32 * q : 32 * q + 4, :].bitcast(I32)
+            )

@@ -26,10 +26,11 @@ def tile_picked_zlayout_gelu_po_kernel(
     nc = tc.nc
     with ExitStack() as ctx:
         keep = ctx.enter_context(tc.tile_pool(name="keep", bufs=1))
+        load = ctx.enter_context(tc.tile_pool(name="load", bufs=1))
         psum = ctx.enter_context(tc.psum_pool(name="psum", bufs=1))
 
-        def sb(name, shape, dtype):
-            return keep.tile(shape, dtype, name=name, align_bytes=64)
+        def sb(name, shape, dtype, tag=None):
+            return keep.tile(shape, dtype, name=name, tag=tag or name, align_bytes=64)
 
         names = ("x", "e", "y")
         words_in = (x_words, e_words, y_words)
@@ -39,16 +40,30 @@ def tile_picked_zlayout_gelu_po_kernel(
         columns = [w.shape[2] for w in words_in]
 
         lists = [sb("list_" + n, [P, TOKENS // 16], U16) for n in names]
-        table_words = [sb("words_" + n, [P, columns[i]], I32) for i, n in enumerate(names)]
-        table_scales = [sb("scales_" + n, [P, columns[i]], U8) for i, n in enumerate(names)]
-        raw = [sb("raw_%d" % i, [P, PACK, WIDTH], F32) for i in range(3)]
-        raw4 = [sb("raw4_%d" % i, [P, PACK, WIDTH // 2], F32) for i in range(2)]
+        KB = 1024
+        early = load.tile([P, 10 * KB], F32, name="early", offset=0, align_bytes=64)
+        word_offset = (0, 8 * KB, 12 * KB)
+        table_words = [
+            load.tile([P, columns[i]], I32, name="words_" + n, offset=word_offset[i], align_bytes=64) for i, n in enumerate(names)
+        ]
+        table_scales = [sb("scales_" + n, [P, columns[i]], U8, "plane_" + n) for i, n in enumerate(names)]
+        raw1 = sb("raw1", [P, PACK, WIDTH], F32)
+        raw2 = load.tile([P, PACK, WIDTH], F32, name="raw2", offset=16 * KB, align_bytes=64)
+        raw3 = [load.tile([P, PACK, WIDTH // 2], F32, name="raw3_%d" % i, offset=(24 + 4 * i) * KB, align_bytes=64) for i in range(2)]
+        cut4 = (0, 128, 384, 512)
+        raw4 = [
+            load.tile([P, PACK, cut4[i + 1] - cut4[i]], F32, name="raw4_%d" % i, offset=32 * KB + 16 * cut4[i], align_bytes=64)
+            for i in range(3)
+        ]
         warm_in = sb("warm_in", [P, 8], F32)
         warm_out = sb("warm_out", [P, 8], F32)
 
-        for i in range(3):
-            nc.vector.memset(table_scales[i][:].bitcast(I32), 0)
-        nc.gpsimd.memset(warm_in[:], 0.0)
+        nc.vector.memset(early[:, 0:8], 0.0)
+        nc.vector.memset(table_scales[1][:].bitcast(I32), 0)
+        nc.vector.tensor_copy(warm_in[:], early[:, 0:8])
+        for i in (0, 2):
+            nc.gpsimd.memset(table_scales[i][:].bitcast(I32), 0)
+        nc.scalar.activation(warm_out[:], warm_in[:], GELU)
 
         def load_weight(dst, w, c0, c1):
             nc.sync.dma_start(out=dst[:], in_=w.rearrange("(p j) c -> p j c", j=PACK)[:, :, c0:c1])
@@ -56,58 +71,89 @@ def tile_picked_zlayout_gelu_po_kernel(
         def load_words(i):
             nc.sync.dma_start(out=table_words[i][:], in_=words_in[i][0].rearrange("p n t -> p (n t)").bitcast(I32))
 
-        def load_scales(i):
-            for q in range(4):
-                p0 = 32 * q + first_row[i]
-                nc.scalar.dma_start(
-                    out=table_scales[i][p0 : p0 + 4, :].bitcast(I32),
-                    in_=scales_in[i][0, 4 * q : 4 * q + 4, :].bitcast(I32),
+        def load_scales(i, queue):
+            for r in range(4):
+                queue.dma_start(
+                    out=table_scales[i][first_row[i] + r : P : 32, :].bitcast(I32),
+                    in_=scales_in[i][0, r:16:4, :].bitcast(I32),
                 )
 
-        load_weight(raw[0], w1, 0, WIDTH)
-        nc.sync.dma_start(lists[0][:], offs)
-        load_scales(0)
-        load_weight(raw[1], w2, 0, WIDTH)
         nc.sync.dma_start(lists[1][:], tok)
+        load_weight(raw1, w1, 0, WIDTH)
+        nc.sync.dma_start(lists[0][:], offs)
         nc.sync.dma_start(lists[2][:], row)
-        load_scales(1)
-        load_scales(2)
-        nc.scalar.activation(warm_out[:], warm_in[:], GELU)
-        load_weight(raw[2], w3, 0, WIDTH)
+        load_scales(1, nc.sync)
+        load_weight(raw2, w2, 0, WIDTH)
+        load_scales(0, nc.sync)
+        load_words(1)
+        load_weight(raw3[0], w3, 0, WIDTH // 2)
+        load_scales(2, nc.sync)
+        load_weight(raw3[1], w3, WIDTH // 2, WIDTH)
+        load_words(0)
+        load_words(2)
         for i in range(3):
-            load_words(i)
-        load_weight(raw4[0], w4, 0, WIDTH // 2)
-        load_weight(raw4[1], w4, WIDTH // 2, WIDTH)
+            load_weight(raw4[i], w4, cut4[i], cut4[i + 1])
 
-        picked_scales = [sb("picked_scales_" + n, [P, TOKENS], U8) for n in names]
-        for i in range(3):
+        picked_scales = {}
+
+        def pick_scales(i):
+            picked_scales[i] = sb("picked_scales_" + names[i], [P, TOKENS], U8, "stage_c" if i == 2 else None)
             nc.vector.tensor_copy(picked_scales[i][:], table_scales[i][:].indirect(lists[i][:]))
 
-        grouped = [sb("grouped_%d" % i, [P, PACK, P, PACK], BF16) for i in range(4)]
-        w_codes = [sb("w_codes_%d" % i, [P, WIDTH], U32) for i in range(4)]
-        w_scales = [sb("w_scales_%d" % i, [P, WIDTH], U8) for i in range(4)]
+        grouped = {}
+        stage_tag = ("stage_a", "stage_c", "stage_b")
+        w_codes = {i: sb("w_codes_%d" % i, [P, WIDTH], U32) for i in (0, 2, 3)}
+        w_scales = {3: sb("w_scales_3", [P, WIDTH], U8)}
 
-        def deal(copy, i, src, m0, m1):
+        def deal(copy, i, src, m0, m1, t0, t1):
+            if i not in grouped:
+                if i >= 2:
+                    place = 44 * KB if i == 3 else 40 * KB
+                    grouped[i] = load.tile([P, PACK, P, PACK], BF16, name="grouped_%d" % i, offset=place, align_bytes=64)
+                else:
+                    grouped[i] = sb("grouped_%d" % i, [P, PACK, P, PACK], BF16, stage_tag[i])
             copy(
-                out=grouped[i][:, :, m0:m1, :].rearrange("p t m j -> p m j t"),
-                in_=src.rearrange("p j (m t) -> p m j t", t=PACK),
+                out=grouped[i][:, t0:t1, m0:m1, :].rearrange("p t m j -> p m j t"),
+                in_=src.rearrange("p j (m t) -> p m j t", t=PACK)[:, :, :, t0:t1],
             )
 
-        def quantize_weight(i):
+        def quantize_weight(i, t0=0, t1=PACK):
             nc.vector.quantize_mx(
-                out=w_codes[i][:].bitcast(FP8X4),
-                scales=w_scales[i][:],
-                in_=grouped[i][:].rearrange("p t m j -> p (t m j)"),
+                out=w_codes[i][:, t0 * P : t1 * P].bitcast(FP8X4),
+                scales=w_scales[i][:, t0 * P : t1 * P],
+                in_=grouped[i][:, t0:t1].rearrange("p t m j -> p (t m j)"),
             )
 
-        for i in range(3):
-            deal(nc.scalar.copy, i, raw[i][:], 0, P)
-            quantize_weight(i)
+        picked = {}
 
-        picked = [sb("picked_" + n, [P, TOKENS], U32) for n in names[:2]]
-        for i in range(2):
+        def pick_words(i):
+            if i == 0:
+                picked[i] = load.tile([P, TOKENS], U32, name="picked_x", offset=40 * KB, align_bytes=64)
+            else:
+                picked[i] = sb("picked_" + names[i], [P, TOKENS], U32, "stage_a")
             nc.vector.tensor_copy(picked[i][:], table_words[i][:].bitcast(U32).indirect(lists[i][:]))
-        picked_y = [sb("picked_y_%d" % c, [P, CHUNK], U32) for c in range(CHUNKS)]
+
+        deal(nc.scalar.copy, 0, raw1[:], 0, P, 0, 2)
+        deal(nc.vector.tensor_copy, 0, raw1[:], 0, P, 2, 4)
+        pick_scales(1)
+        w_scales[0] = sb("w_scales_0", [P, WIDTH], U8, "plane_e")
+        quantize_weight(0)
+        deal(nc.scalar.copy, 1, raw2[:], 0, P, 0, 4)
+        pick_scales(0)
+        pick_words(1)
+        w_scales[1] = sb("w_scales_1", [P, WIDTH], U8, "plane_x")
+        w_codes[1] = load.tile([P, WIDTH], U32, name="w_codes_1", offset=word_offset[1], align_bytes=64)
+        quantize_weight(1)
+        deal(nc.scalar.copy, 2, raw3[0][:], 0, P // 2, 0, 4)
+        deal(nc.scalar.copy, 2, raw3[1][:], P // 2, P, 0, 4)
+        pick_scales(2)
+        w_scales[2] = sb("w_scales_2", [P, WIDTH], U8, "plane_y")
+        quantize_weight(2)
+        pick_words(0)
+        picked_y = [
+            load.tile([P, CHUNK], U32, name="picked_y_%d" % c, offset=42 * KB + 4 * CHUNK * c, align_bytes=64)
+            for c in range(CHUNKS)
+        ]
         for c in range(CHUNKS):
             nc.vector.tensor_copy(
                 picked_y[c][:], table_words[2][:].bitcast(U32).indirect(lists[2][:, c * CHUNK // 16 : (c + 1) * CHUNK // 16])
@@ -126,40 +172,59 @@ def tile_picked_zlayout_gelu_po_kernel(
                 lhsT_scale=w_scales[i][:, slot],
                 rhs=codes.bitcast(FP8X4),
                 rhs_scale=picked_scales[i][first_row[i] : P, cols],
-                start=(i == 0),
+                start=(i == 1),
                 stop=(i == 2),
             )
 
-        for i in range(2):
-            for c in range(CHUNKS):
-                first_layer_pass(i, c, 0)
+        for c in range(CHUNKS):
+            first_layer_pass(1, c, 0)
+        for c in range(CHUNKS):
+            nc.tensor.matmul_mx(
+                out=result[c][:].rearrange("p t n -> p (t n)"),
+                lhsT=w_codes[0][:, 0:P].bitcast(FP8X4),
+                lhsT_scale=w_scales[0][:, 0:P],
+                rhs=(picked[1] if c < 2 else w_codes[2])[:].bitcast(FP8X4),
+                rhs_scale=picked_scales[2][first_row[2] : P, :] if c < 2 else w_scales[2][:],
+                start=True,
+                stop=True,
+            )
 
-        h_bf = [sb("h_bf_%d" % c, [P, CHUNK, PACK], BF16) for c in range(CHUNKS)]
-        h_codes = [sb("h_codes_%d" % c, [P, CHUNK], U32) for c in range(CHUNKS)]
+        for c in range(CHUNKS):
+            first_layer_pass(0, c, 0)
+
+        deal(nc.scalar.copy, 3, raw4[0][:], 0, 32, 0, 4)
+        h_bf = [load.tile([P, CHUNK, PACK], BF16, name="h_bf_0", offset=32 * KB, align_bytes=64)]
+        h_bf.extend(sb("h_bf_%d" % c, [P, CHUNK, PACK], BF16) for c in range(1, CHUNKS))
+        h_place = (38 * KB, 44 * KB, 44 * KB + 4 * CHUNK, 44 * KB + 8 * CHUNK)
+        h_codes = [load.tile([P, CHUNK], U32, name="h_codes_%d" % c, offset=h_place[c], align_bytes=64) for c in range(CHUNKS)]
         h_scales = [sb("h_scales_%d" % c, [P, CHUNK], U8) for c in range(CHUNKS)]
         for c in range(CHUNKS):
             first_layer_pass(2, c, 0)
             for t in range(1, PACK):
-                for i in range(3):
+                for i in (1, 0, 2):
                     first_layer_pass(i, c, t)
             nc.scalar.activation(h_bf[c][:], hidden[c][:].rearrange("p t n -> p n t"), GELU)
 
-        deal(nc.vector.tensor_copy, 3, raw4[0][:], 0, P // 2)
-        deal(nc.vector.tensor_copy, 3, raw4[1][:], P // 2, P)
-        quantize_weight(3)
-        for c in range(CHUNKS):
+        def quantize_hidden(c):
             nc.vector.quantize_mx(
                 out=h_codes[c][:].bitcast(FP8X4), scales=h_scales[c][:], in_=h_bf[c][:].rearrange("p n t -> p (n t)")
             )
 
+        deal(nc.vector.tensor_copy, 3, raw4[1][:], 32, 96, 0, 4)
+        deal(nc.vector.tensor_copy, 3, raw4[2][:], 96, P, 0, 4)
+        quantize_hidden(0)
+        quantize_weight(3, 0, 2)
+        quantize_weight(3, 2, 4)
+        for c in range(1, CHUNKS):
+            quantize_hidden(c)
+
         out_f32 = [sb("out_f32_%d" % c, [P, PACK, CHUNK], F32) for c in range(CHUNKS)]
-        out_bf = [sb("out_bf_%d" % c, [P, CHUNK, PACK], BF16) for c in range(CHUNKS)]
+        out_bf = [sb("out_bf_%d" % h, [P, 2, CHUNK, PACK], BF16) for h in range(2)]
         out_codes = sb("out_codes", [P, TOKENS], U32)
         out_scales = sb("out_scales", [P, TOKENS], U8)
         out_rows = out_0.rearrange("(p t) n -> p t n", t=PACK)
         out_words = out_1[0].rearrange("p n t -> p (n t)").bitcast(I32)
         for c in range(CHUNKS):
-            cols = slice(c * CHUNK, (c + 1) * CHUNK)
             for t in range(PACK):
                 slot = slice(t * P, (t + 1) * P)
                 nc.tensor.matmul_mx(
@@ -171,22 +236,41 @@ def tile_picked_zlayout_gelu_po_kernel(
                     start=True,
                     stop=True,
                 )
+
+        def store_rows(c):
             nc.scalar.copy(out=out_f32[c][:], in_=result[c][:])
-            nc.sync.dma_start(out=out_rows[:, :, cols], in_=out_f32[c][:])
+            nc.sync.dma_start(out=out_rows[:, :, c * CHUNK : (c + 1) * CHUNK], in_=out_f32[c][:])
+
+        def round_from_bank(c):
+            nc.vector.tensor_copy(out=out_bf[c // 2][:, c % 2], in_=result[c][:].rearrange("p t n -> p n t"))
+
+        def round_from_copy(c):
             nc.vector.tensor_copy(
-                out=out_bf[c][:].rearrange("p (a b) t -> p a t b", b=4),
+                out=out_bf[c // 2][:, c % 2].rearrange("p (a b) t -> p a t b", b=4),
                 in_=out_f32[c][:].rearrange("p t (a b) -> p a t b", b=4),
             )
+
+        def store_codes(h):
+            pair = slice(2 * h * CHUNK, (2 * h + 2) * CHUNK)
             nc.vector.quantize_mx(
-                out=out_codes[:, cols].bitcast(FP8X4),
-                scales=out_scales[:, cols],
-                in_=out_bf[c][:].rearrange("p n t -> p (n t)"),
+                out=out_codes[:, pair].bitcast(FP8X4),
+                scales=out_scales[:, pair],
+                in_=out_bf[h][:].rearrange("p c n t -> p (c n t)"),
             )
-            if c % 2 == 1:
-                pair = slice((c - 1) * CHUNK, (c + 1) * CHUNK)
-                nc.sync.dma_start(out=out_words[:, pair], in_=out_codes[:, pair].bitcast(I32))
+            nc.sync.dma_start(out=out_words[:, pair], in_=out_codes[:, pair].bitcast(I32))
+
+        store_rows(0)
+        round_from_bank(1)
+        store_rows(2)
+        round_from_bank(3)
+        store_rows(1)
+        round_from_copy(0)
+        round_from_copy(2)
+        store_codes(0)
+        store_rows(3)
+        store_codes(1)
         for q in range(4):
             queue = nc.scalar if q % 2 else nc.sync
             queue.dma_start(
-                out=out_2[0, 4 * q : 4 * q + 4, :].bitcast(I32), in_=out_scales[32 * q : 32 * q + 4, :].bitcast(I32)
+                out=out_2[0, q:16:4, :].bitcast(I32), in_=out_scales[q:P:32, :].bitcast(I32)
             )

@@ -26,44 +26,44 @@ def tile_picked_zlayout_gelu_po_kernel(
     nc = tc.nc
     with ExitStack() as ctx:
         keep = ctx.enter_context(tc.tile_pool(name="keep", bufs=1))
-        load = ctx.enter_context(tc.tile_pool(name="load", bufs=1))
+        late = ctx.enter_context(tc.tile_pool(name="late", bufs=1))
         psum = ctx.enter_context(tc.psum_pool(name="psum", bufs=1))
 
-        def sb(name, shape, dtype, tag=None):
-            return keep.tile(shape, dtype, name=name, tag=tag or name, align_bytes=64)
+        def sb(name, shape, dtype):
+            return keep.tile(shape, dtype, name=name, align_bytes=64)
 
         names = ("x", "e", "y")
         words_in = (x_words, e_words, y_words)
         scales_in = (x_scales, e_scales, y_scales)
         lists_in = (offs, tok, row)
-        first_row = (0, 4, 8)
         columns = [w.shape[2] for w in words_in]
 
         lists = [sb("list_" + n, [P, TOKENS // 16], U16) for n in names]
         KB = 1024
-        early = load.tile([P, 10 * KB], F32, name="early", offset=0, align_bytes=64)
-        word_offset = (0, 8 * KB, 12 * KB)
+        held = late.tile([P, 21 * KB], U8, name="scales_e", offset=0, align_bytes=64)
         table_words = [
-            load.tile([P, columns[i]], I32, name="words_" + n, offset=word_offset[i], align_bytes=64) for i, n in enumerate(names)
+            late.tile([P, columns[0]], I32, name="words_x", offset=KB, align_bytes=64),
+            sb("words_e", [P, columns[1]], I32),
+            late.tile([P, columns[2]], I32, name="words_y", offset=9 * KB, align_bytes=64),
         ]
-        table_scales = [sb("scales_" + n, [P, columns[i]], U8, "plane_" + n) for i, n in enumerate(names)]
-        raw1 = sb("raw1", [P, PACK, WIDTH], F32)
-        raw2 = load.tile([P, PACK, WIDTH], F32, name="raw2", offset=16 * KB, align_bytes=64)
-        raw3 = [load.tile([P, PACK, WIDTH // 2], F32, name="raw3_%d" % i, offset=(24 + 4 * i) * KB, align_bytes=64) for i in range(2)]
+        table_scales = [sb("scales_x", [P, columns[0]], U8)[:], held[:, 0 : columns[1]], sb("scales_y", [P, columns[2]], U8)[:]]
+        picked_rows = sb("picked_rows", [P, 3 * TOKENS], U8)
+        planes = sb("planes", [P, 3 * TOKENS], U8)
+        raw = [sb("raw_%d" % i, [P, PACK, WIDTH], F32) for i in range(3)]
         cut4 = (0, 128, 384, 512)
         raw4 = [
-            load.tile([P, PACK, cut4[i + 1] - cut4[i]], F32, name="raw4_%d" % i, offset=32 * KB + 16 * cut4[i], align_bytes=64)
+            late.tile([P, PACK, cut4[i + 1] - cut4[i]], F32, name="raw4_%d" % i, offset=13 * KB + 16 * cut4[i], align_bytes=64)
             for i in range(3)
         ]
         warm_in = sb("warm_in", [P, 8], F32)
         warm_out = sb("warm_out", [P, 8], F32)
 
-        nc.vector.memset(early[:, 0:8], 0.0)
-        nc.vector.memset(table_scales[1][:].bitcast(I32), 0)
-        nc.vector.tensor_copy(warm_in[:], early[:, 0:8])
-        for i in (0, 2):
-            nc.gpsimd.memset(table_scales[i][:].bitcast(I32), 0)
-        nc.scalar.activation(warm_out[:], warm_in[:], GELU)
+        ROWS = P - 16
+        nc.vector.memset(warm_in[:], 0.0)
+        nc.vector.memset(table_scales[0][0:ROWS, :].bitcast(I32), 0)
+        nc.vector.memset(table_scales[2][0:ROWS, :].bitcast(I32), 0)
+        nc.vector.memset(table_scales[1][0:ROWS, :].bitcast(I32), 0)
+        nc.vector.memset(planes[:].bitcast(I32), 0)
 
         def load_weight(dst, w, c0, c1):
             nc.sync.dma_start(out=dst[:], in_=w.rearrange("(p j) c -> p j c", j=PACK)[:, :, c0:c1])
@@ -71,47 +71,30 @@ def tile_picked_zlayout_gelu_po_kernel(
         def load_words(i):
             nc.sync.dma_start(out=table_words[i][:], in_=words_in[i][0].rearrange("p n t -> p (n t)").bitcast(I32))
 
-        def load_scales(i, queue):
-            for r in range(4):
-                queue.dma_start(
-                    out=table_scales[i][first_row[i] + r : P : 32, :].bitcast(I32),
-                    in_=scales_in[i][0, r:16:4, :].bitcast(I32),
-                )
-
-        nc.sync.dma_start(lists[1][:], tok)
-        load_weight(raw1, w1, 0, WIDTH)
-        nc.sync.dma_start(lists[0][:], offs)
-        nc.sync.dma_start(lists[2][:], row)
-        load_scales(1, nc.sync)
-        load_weight(raw2, w2, 0, WIDTH)
-        load_scales(0, nc.sync)
         load_words(1)
-        load_weight(raw3[0], w3, 0, WIDTH // 2)
-        load_scales(2, nc.sync)
-        load_weight(raw3[1], w3, WIDTH // 2, WIDTH)
+        for i in (0, 2, 1):
+            nc.sync.dma_start(lists[i][:], lists_in[i])
+        for i in (0, 2, 1):
+            nc.scalar.dma_start(out=table_scales[i][ROWS:P, :].bitcast(I32), in_=scales_in[i][0].bitcast(I32))
+        nc.scalar.activation(warm_out[:], warm_in[:], GELU)
+        load_weight(raw[1], w2, 0, WIDTH)
+        load_weight(raw[0], w1, 0, WIDTH)
+        load_weight(raw[2], w3, 0, WIDTH)
+
+        for i in (0, 2, 1):
+            nc.vector.tensor_copy(picked_rows[:, i * TOKENS : (i + 1) * TOKENS], table_scales[i].indirect(lists[i][:]))
+        for r in range(4):
+            nc.sync.dma_start(out=planes[r:P:32, :].bitcast(I32), in_=picked_rows[ROWS + r : P : 4, :].bitcast(I32))
         load_words(0)
         load_words(2)
         for i in range(3):
             load_weight(raw4[i], w4, cut4[i], cut4[i + 1])
 
-        picked_scales = {}
-
-        def pick_scales(i):
-            picked_scales[i] = sb("picked_scales_" + names[i], [P, TOKENS], U8, "stage_c" if i == 2 else None)
-            nc.vector.tensor_copy(picked_scales[i][:], table_scales[i][:].indirect(lists[i][:]))
-
-        grouped = {}
-        stage_tag = ("stage_a", "stage_c", "stage_b")
-        w_codes = {i: sb("w_codes_%d" % i, [P, WIDTH], U32) for i in (0, 2, 3)}
-        w_scales = {3: sb("w_scales_3", [P, WIDTH], U8)}
+        grouped = [sb("grouped_%d" % i, [P, PACK, P, PACK], BF16) for i in range(4)]
+        w_codes = [sb("w_codes_%d" % i, [P, WIDTH], U32) for i in range(4)]
+        w_scales = [sb("w_scales_%d" % i, [P, WIDTH], U8) for i in range(4)]
 
         def deal(copy, i, src, m0, m1, t0, t1):
-            if i not in grouped:
-                if i >= 2:
-                    place = 44 * KB if i == 3 else 40 * KB
-                    grouped[i] = load.tile([P, PACK, P, PACK], BF16, name="grouped_%d" % i, offset=place, align_bytes=64)
-                else:
-                    grouped[i] = sb("grouped_%d" % i, [P, PACK, P, PACK], BF16, stage_tag[i])
             copy(
                 out=grouped[i][:, t0:t1, m0:m1, :].rearrange("p t m j -> p m j t"),
                 in_=src.rearrange("p j (m t) -> p m j t", t=PACK)[:, :, :, t0:t1],
@@ -124,36 +107,22 @@ def tile_picked_zlayout_gelu_po_kernel(
                 in_=grouped[i][:, t0:t1].rearrange("p t m j -> p (t m j)"),
             )
 
-        picked = {}
+        picked = [sb("picked_" + names[i], [P, TOKENS], U32) for i in range(2)]
+        picked_y = [sb("picked_y_%d" % c, [P, CHUNK], U32) for c in range(CHUNKS)]
 
         def pick_words(i):
-            if i == 0:
-                picked[i] = load.tile([P, TOKENS], U32, name="picked_x", offset=40 * KB, align_bytes=64)
-            else:
-                picked[i] = sb("picked_" + names[i], [P, TOKENS], U32, "stage_a")
             nc.vector.tensor_copy(picked[i][:], table_words[i][:].bitcast(U32).indirect(lists[i][:]))
 
-        deal(nc.scalar.copy, 0, raw1[:], 0, P, 0, 2)
-        deal(nc.vector.tensor_copy, 0, raw1[:], 0, P, 2, 4)
-        pick_scales(1)
-        w_scales[0] = sb("w_scales_0", [P, WIDTH], U8, "plane_e")
-        quantize_weight(0)
-        deal(nc.scalar.copy, 1, raw2[:], 0, P, 0, 4)
-        pick_scales(0)
         pick_words(1)
-        w_scales[1] = sb("w_scales_1", [P, WIDTH], U8, "plane_x")
-        w_codes[1] = load.tile([P, WIDTH], U32, name="w_codes_1", offset=word_offset[1], align_bytes=64)
+        deal(nc.scalar.copy, 1, raw[1][:], 0, P, 0, 4)
+        deal(nc.scalar.copy, 0, raw[0][:], 0, P, 0, 2)
+        deal(nc.vector.tensor_copy, 0, raw[0][:], 0, P, 2, 4)
         quantize_weight(1)
-        deal(nc.scalar.copy, 2, raw3[0][:], 0, P // 2, 0, 4)
-        deal(nc.scalar.copy, 2, raw3[1][:], P // 2, P, 0, 4)
-        pick_scales(2)
-        w_scales[2] = sb("w_scales_2", [P, WIDTH], U8, "plane_y")
+        quantize_weight(0)
+        deal(nc.scalar.copy, 2, raw[2][:], 0, P, 0, 2)
+        deal(nc.vector.tensor_copy, 2, raw[2][:], 0, P, 2, 4)
         quantize_weight(2)
         pick_words(0)
-        picked_y = [
-            load.tile([P, CHUNK], U32, name="picked_y_%d" % c, offset=42 * KB + 4 * CHUNK * c, align_bytes=64)
-            for c in range(CHUNKS)
-        ]
         for c in range(CHUNKS):
             nc.vector.tensor_copy(
                 picked_y[c][:], table_words[2][:].bitcast(U32).indirect(lists[2][:, c * CHUNK // 16 : (c + 1) * CHUNK // 16])
@@ -171,7 +140,7 @@ def tile_picked_zlayout_gelu_po_kernel(
                 lhsT=w_codes[i][:, slot].bitcast(FP8X4),
                 lhsT_scale=w_scales[i][:, slot],
                 rhs=codes.bitcast(FP8X4),
-                rhs_scale=picked_scales[i][first_row[i] : P, cols],
+                rhs_scale=planes[:, i * TOKENS + c * CHUNK : i * TOKENS + (c + 1) * CHUNK],
                 start=(i == 1),
                 stop=(i == 2),
             )
@@ -183,8 +152,8 @@ def tile_picked_zlayout_gelu_po_kernel(
                 out=result[c][:].rearrange("p t n -> p (t n)"),
                 lhsT=w_codes[0][:, 0:P].bitcast(FP8X4),
                 lhsT_scale=w_scales[0][:, 0:P],
-                rhs=(picked[1] if c < 2 else w_codes[2])[:].bitcast(FP8X4),
-                rhs_scale=picked_scales[2][first_row[2] : P, :] if c < 2 else w_scales[2][:],
+                rhs=w_codes[1 if c < 2 else 2][:].bitcast(FP8X4),
+                rhs_scale=w_scales[1 if c < 2 else 2][:],
                 start=True,
                 stop=True,
             )
@@ -193,10 +162,8 @@ def tile_picked_zlayout_gelu_po_kernel(
             first_layer_pass(0, c, 0)
 
         deal(nc.scalar.copy, 3, raw4[0][:], 0, 32, 0, 4)
-        h_bf = [load.tile([P, CHUNK, PACK], BF16, name="h_bf_0", offset=32 * KB, align_bytes=64)]
-        h_bf.extend(sb("h_bf_%d" % c, [P, CHUNK, PACK], BF16) for c in range(1, CHUNKS))
-        h_place = (38 * KB, 44 * KB, 44 * KB + 4 * CHUNK, 44 * KB + 8 * CHUNK)
-        h_codes = [load.tile([P, CHUNK], U32, name="h_codes_%d" % c, offset=h_place[c], align_bytes=64) for c in range(CHUNKS)]
+        h_bf = [sb("h_bf_%d" % c, [P, CHUNK, PACK], BF16) for c in range(CHUNKS)]
+        h_codes = [sb("h_codes_%d" % c, [P, CHUNK], U32) for c in range(CHUNKS)]
         h_scales = [sb("h_scales_%d" % c, [P, CHUNK], U8) for c in range(CHUNKS)]
         for c in range(CHUNKS):
             first_layer_pass(2, c, 0)
@@ -237,12 +204,9 @@ def tile_picked_zlayout_gelu_po_kernel(
                     stop=True,
                 )
 
-        def store_rows(c):
-            nc.scalar.copy(out=out_f32[c][:], in_=result[c][:])
+        def store_rows(c, copy):
+            copy(out=out_f32[c][:], in_=result[c][:])
             nc.sync.dma_start(out=out_rows[:, :, c * CHUNK : (c + 1) * CHUNK], in_=out_f32[c][:])
-
-        def round_from_bank(c):
-            nc.vector.tensor_copy(out=out_bf[c // 2][:, c % 2], in_=result[c][:].rearrange("p t n -> p n t"))
 
         def round_from_copy(c):
             nc.vector.tensor_copy(
@@ -259,15 +223,15 @@ def tile_picked_zlayout_gelu_po_kernel(
             )
             nc.sync.dma_start(out=out_words[:, pair], in_=out_codes[:, pair].bitcast(I32))
 
-        store_rows(0)
-        round_from_bank(1)
-        store_rows(2)
-        round_from_bank(3)
-        store_rows(1)
+        store_rows(0, nc.vector.tensor_copy)
+        store_rows(1, nc.scalar.copy)
         round_from_copy(0)
-        round_from_copy(2)
+        store_rows(2, nc.scalar.copy)
+        round_from_copy(1)
         store_codes(0)
-        store_rows(3)
+        round_from_copy(2)
+        store_rows(3, nc.scalar.copy)
+        round_from_copy(3)
         store_codes(1)
         for q in range(4):
             queue = nc.scalar if q % 2 else nc.sync

@@ -128,15 +128,17 @@ def tile_picked_zlayout_gelu_po_kernel(
                 picked_y[c][:], table_words[2][:].bitcast(U32).indirect(lists[2][:, c * CHUNK // 16 : (c + 1) * CHUNK // 16])
             )
 
-        hidden = [psum.tile([P, PACK, CHUNK], F32, name="hidden_%d" % c) for c in range(CHUNKS)]
-        result = [psum.tile([P, PACK, CHUNK], F32, name="result_%d" % c) for c in range(CHUNKS)]
+        BANK = 2048
+        first = [psum.tile([P, CHUNK], F32, name="first_%d" % t, offset=t * BANK) for t in range(PACK)]
+        hidden = {c: psum.tile([P, PACK, CHUNK], F32, name="hidden_%d" % c, offset=(3 + c) * BANK) for c in range(1, CHUNKS)}
+        result = [psum.tile([P, PACK, CHUNK], F32, name="result_%d" % c, offset=((c - 1) % 8) * BANK) for c in range(CHUNKS)]
 
         def first_layer_pass(i, c, t):
             cols = slice(c * CHUNK, (c + 1) * CHUNK)
             slot = slice(t * P, (t + 1) * P)
             codes = picked_y[c][:] if i == 2 else picked[i][:, cols]
             nc.tensor.matmul_mx(
-                out=hidden[c][:, t, :],
+                out=hidden[c][:, t, :] if c else first[t][:],
                 lhsT=w_codes[i][:, slot].bitcast(FP8X4),
                 lhsT_scale=w_scales[i][:, slot],
                 rhs=codes.bitcast(FP8X4),
@@ -145,11 +147,12 @@ def tile_picked_zlayout_gelu_po_kernel(
                 stop=(i == 2),
             )
 
-        for c in range(CHUNKS):
-            first_layer_pass(1, c, 0)
+        early = [(0, t) for t in range(PACK)] + [(c, 0) for c in range(1, CHUNKS)]
+        for c, t in early:
+            first_layer_pass(1, c, t)
         for c in range(CHUNKS):
             nc.tensor.matmul_mx(
-                out=result[c][:].rearrange("p t n -> p (t n)"),
+                out=result[0][:].rearrange("p t n -> p (t n)"),
                 lhsT=w_codes[0][:, 0:P].bitcast(FP8X4),
                 lhsT_scale=w_scales[0][:, 0:P],
                 rhs=w_codes[1 if c < 2 else 2][:].bitcast(FP8X4),
@@ -158,14 +161,16 @@ def tile_picked_zlayout_gelu_po_kernel(
                 stop=True,
             )
 
-        for c in range(CHUNKS):
-            first_layer_pass(0, c, 0)
+        for c, t in early:
+            first_layer_pass(0, c, t)
 
         deal(nc.scalar.copy, 3, raw4[0][:], 0, 32, 0, 4)
+        h_rows = late.tile([P, PACK, CHUNK], BF16, name="h_rows", offset=13 * KB, align_bytes=64)
         h_bf = [sb("h_bf_%d" % c, [P, CHUNK, PACK], BF16) for c in range(CHUNKS)]
         h_codes = [sb("h_codes_%d" % c, [P, CHUNK], U32) for c in range(CHUNKS)]
         h_scales = [sb("h_scales_%d" % c, [P, CHUNK], U8) for c in range(CHUNKS)]
-        for c in range(CHUNKS):
+
+        def first_layer(c):
             first_layer_pass(2, c, 0)
             for t in range(1, PACK):
                 for i in (1, 0, 2):
@@ -177,21 +182,14 @@ def tile_picked_zlayout_gelu_po_kernel(
                 out=h_codes[c][:].bitcast(FP8X4), scales=h_scales[c][:], in_=h_bf[c][:].rearrange("p n t -> p (n t)")
             )
 
-        deal(nc.vector.tensor_copy, 3, raw4[1][:], 32, 96, 0, 4)
-        deal(nc.vector.tensor_copy, 3, raw4[2][:], 96, P, 0, 4)
-        quantize_hidden(0)
-        quantize_weight(3, 0, 2)
-        quantize_weight(3, 2, 4)
-        for c in range(1, CHUNKS):
-            quantize_hidden(c)
-
         out_f32 = [sb("out_f32_%d" % c, [P, PACK, CHUNK], F32) for c in range(CHUNKS)]
         out_bf = [sb("out_bf_%d" % h, [P, 2, CHUNK, PACK], BF16) for h in range(2)]
         out_codes = sb("out_codes", [P, TOKENS], U32)
         out_scales = sb("out_scales", [P, TOKENS], U8)
         out_rows = out_0.rearrange("(p t) n -> p t n", t=PACK)
         out_words = out_1[0].rearrange("p n t -> p (n t)").bitcast(I32)
-        for c in range(CHUNKS):
+
+        def second_layer(c):
             for t in range(PACK):
                 slot = slice(t * P, (t + 1) * P)
                 nc.tensor.matmul_mx(
@@ -204,8 +202,8 @@ def tile_picked_zlayout_gelu_po_kernel(
                     stop=True,
                 )
 
-        def store_rows(c, copy):
-            copy(out=out_f32[c][:], in_=result[c][:])
+        def store_rows(c):
+            nc.scalar.copy(out=out_f32[c][:], in_=result[c][:])
             nc.sync.dma_start(out=out_rows[:, :, c * CHUNK : (c + 1) * CHUNK], in_=out_f32[c][:])
 
         def round_from_copy(c):
@@ -214,24 +212,52 @@ def tile_picked_zlayout_gelu_po_kernel(
                 in_=out_f32[c][:].rearrange("p t (a b) -> p a t b", b=4),
             )
 
+        def round_from_bank(c):
+            nc.vector.tensor_copy(out=out_bf[c // 2][:, c % 2], in_=result[c][:].rearrange("p t n -> p n t"))
+
+        def quantize_out(c0, c1):
+            cols = slice(c0 * CHUNK, c1 * CHUNK)
+            nc.vector.quantize_mx(
+                out=out_codes[:, cols].bitcast(FP8X4),
+                scales=out_scales[:, cols],
+                in_=out_bf[c0 // 2][:, c0 % 2 : c0 % 2 + c1 - c0].rearrange("p c n t -> p (c n t)"),
+            )
+
         def store_codes(h):
             pair = slice(2 * h * CHUNK, (2 * h + 2) * CHUNK)
-            nc.vector.quantize_mx(
-                out=out_codes[:, pair].bitcast(FP8X4),
-                scales=out_scales[:, pair],
-                in_=out_bf[h][:].rearrange("p c n t -> p (c n t)"),
-            )
             nc.sync.dma_start(out=out_words[:, pair], in_=out_codes[:, pair].bitcast(I32))
 
-        store_rows(0, nc.vector.tensor_copy)
-        store_rows(1, nc.scalar.copy)
+        for t in range(PACK):
+            first_layer_pass(2, 0, t)
+            nc.scalar.activation(h_rows[:, t, :], first[t][:], GELU)
+        first_layer(1)
+        first_layer(2)
+        deal(nc.vector.tensor_copy, 3, raw4[1][:], 32, 96, 0, 4)
+        nc.vector.tensor_copy(
+            out=h_bf[0][:].rearrange("p (a b) t -> p a t b", b=4), in_=h_rows[:].rearrange("p t (a b) -> p a t b", b=4)
+        )
+        deal(nc.vector.tensor_copy, 3, raw4[2][:], 96, P, 0, 4)
+        quantize_hidden(0)
+        quantize_weight(3, 0, 2)
+        quantize_weight(3, 2, 4)
+        second_layer(0)
+        quantize_hidden(1)
+        quantize_hidden(2)
+        first_layer(3)
+        store_rows(0)
+        quantize_hidden(3)
+        for c in range(1, CHUNKS):
+            second_layer(c)
+        round_from_bank(1)
+        store_rows(2)
         round_from_copy(0)
-        store_rows(2, nc.scalar.copy)
-        round_from_copy(1)
-        store_codes(0)
+        round_from_bank(3)
+        store_rows(1)
         round_from_copy(2)
-        store_rows(3, nc.scalar.copy)
-        round_from_copy(3)
+        quantize_out(0, 2)
+        store_codes(0)
+        store_rows(3)
+        quantize_out(2, 4)
         store_codes(1)
         for q in range(4):
             queue = nc.scalar if q % 2 else nc.sync

@@ -42,7 +42,7 @@ def tile_picked_zlayout_gelu_po_kernel(
         KB = 1024
         held = late.tile([P, 21 * KB], U8, name="scales_e", offset=0, align_bytes=64)
         table_words = [
-            late.tile([P, columns[0]], I32, name="words_x", offset=KB, align_bytes=64),
+            sb("words_x", [P, columns[0]], I32),
             sb("words_e", [P, columns[1]], I32),
             late.tile([P, columns[2]], I32, name="words_y", offset=9 * KB, align_bytes=64),
         ]
@@ -80,12 +80,12 @@ def tile_picked_zlayout_gelu_po_kernel(
         load_weight(raw[1], w2, 0, WIDTH)
         load_weight(raw[0], w1, 0, WIDTH)
         load_weight(raw[2], w3, 0, WIDTH)
+        load_words(0)
 
         for i in (0, 2, 1):
             nc.vector.tensor_copy(picked_rows[:, i * TOKENS : (i + 1) * TOKENS], table_scales[i].indirect(lists[i][:]))
         for r in range(4):
             nc.sync.dma_start(out=planes[r:P:32, :].bitcast(I32), in_=picked_rows[ROWS + r : P : 4, :].bitcast(I32))
-        load_words(0)
         load_words(2)
         for i in range(3):
             load_weight(raw4[i], w4, cut4[i], cut4[i + 1])
@@ -260,7 +260,7 @@ def tile_picked_zlayout_gelu_po_kernel(
         quantize_out(2, 4)
         store_codes(1)
         for q in range(4):
-            queue = nc.scalar if q % 2 else nc.sync
+            queue = nc.scalar if q else nc.sync
             queue.dma_start(
                 out=out_2[0, q:16:4, :].bitcast(I32), in_=out_scales[q:P:32, :].bitcast(I32)
             )

@@ -131,7 +131,7 @@ def tile_picked_zlayout_gelu_po_kernel(
         BANK = 2048
         first = [psum.tile([P, CHUNK], F32, name="first_%d" % t, offset=t * BANK) for t in range(PACK)]
         hidden = {c: psum.tile([P, PACK, CHUNK], F32, name="hidden_%d" % c, offset=(3 + c) * BANK) for c in range(1, CHUNKS)}
-        result = [psum.tile([P, PACK, CHUNK], F32, name="result_%d" % c, offset=((c - 1) % 8) * BANK) for c in range(CHUNKS)]
+        result = [psum.tile([P, 2, 2 * CHUNK], F32, name="result_%d" % b, offset=((b - 1) % 8) * BANK) for b in range(4)]
 
         def first_layer_pass(i, c, t):
             cols = slice(c * CHUNK, (c + 1) * CHUNK)
@@ -167,8 +167,8 @@ def tile_picked_zlayout_gelu_po_kernel(
         deal(nc.scalar.copy, 3, raw4[0][:], 0, 32, 0, 4)
         h_rows = late.tile([P, PACK, CHUNK], BF16, name="h_rows", offset=13 * KB, align_bytes=64)
         h_bf = [sb("h_bf_%d" % c, [P, CHUNK, PACK], BF16) for c in range(CHUNKS)]
-        h_codes = [sb("h_codes_%d" % c, [P, CHUNK], U32) for c in range(CHUNKS)]
-        h_scales = [sb("h_scales_%d" % c, [P, CHUNK], U8) for c in range(CHUNKS)]
+        h_codes = sb("h_codes", [P, TOKENS], U32)
+        h_scales = sb("h_scales", [P, TOKENS], U8)
 
         def first_layer(c):
             first_layer_pass(2, c, 0)
@@ -179,41 +179,43 @@ def tile_picked_zlayout_gelu_po_kernel(
 
         def quantize_hidden(c):
             nc.vector.quantize_mx(
-                out=h_codes[c][:].bitcast(FP8X4), scales=h_scales[c][:], in_=h_bf[c][:].rearrange("p n t -> p (n t)")
+                out=h_codes[:, c * CHUNK : (c + 1) * CHUNK].bitcast(FP8X4),
+                scales=h_scales[:, c * CHUNK : (c + 1) * CHUNK],
+                in_=h_bf[c][:].rearrange("p n t -> p (n t)"),
             )
 
-        out_f32 = [sb("out_f32_%d" % c, [P, PACK, CHUNK], F32) for c in range(CHUNKS)]
+        out_f32 = [sb("out_f32_%d" % h, [P, PACK, 2 * CHUNK], F32) for h in range(2)]
         out_bf = [sb("out_bf_%d" % h, [P, 2, CHUNK, PACK], BF16) for h in range(2)]
         out_codes = sb("out_codes", [P, TOKENS], U32)
         out_scales = sb("out_scales", [P, TOKENS], U8)
         out_rows = out_0.rearrange("(p t) n -> p t n", t=PACK)
         out_words = out_1[0].rearrange("p n t -> p (n t)").bitcast(I32)
 
-        def second_layer(c):
+        def second_layer(h):
+            half = slice(2 * h * CHUNK, (2 * h + 2) * CHUNK)
             for t in range(PACK):
                 slot = slice(t * P, (t + 1) * P)
                 nc.tensor.matmul_mx(
-                    out=result[c][:, t, :],
+                    out=result[2 * h + t // 2][:, t % 2, :],
                     lhsT=w_codes[3][:, slot].bitcast(FP8X4),
                     lhsT_scale=w_scales[3][:, slot],
-                    rhs=h_codes[c][:].bitcast(FP8X4),
-                    rhs_scale=h_scales[c][:],
+                    rhs=h_codes[:, half].bitcast(FP8X4),
+                    rhs_scale=h_scales[:, half],
                     start=True,
                     stop=True,
                 )
 
-        def store_rows(c):
-            nc.scalar.copy(out=out_f32[c][:], in_=result[c][:])
-            nc.sync.dma_start(out=out_rows[:, :, c * CHUNK : (c + 1) * CHUNK], in_=out_f32[c][:])
-
-        def round_from_copy(c):
-            nc.vector.tensor_copy(
-                out=out_bf[c // 2][:, c % 2].rearrange("p (a b) t -> p a t b", b=4),
-                in_=out_f32[c][:].rearrange("p t (a b) -> p a t b", b=4),
+        def store_rows(h, u, copy):
+            copy(out=out_f32[h][:, 2 * u : 2 * u + 2, :], in_=result[2 * h + u][:])
+            nc.sync.dma_start(
+                out=out_rows[:, 2 * u : 2 * u + 2, 2 * h * CHUNK : (2 * h + 2) * CHUNK], in_=out_f32[h][:, 2 * u : 2 * u + 2, :]
             )
 
-        def round_from_bank(c):
-            nc.vector.tensor_copy(out=out_bf[c // 2][:, c % 2], in_=result[c][:].rearrange("p t n -> p n t"))
+        def round_from_copy(c, copy):
+            copy(
+                out=out_bf[c // 2][:, c % 2].rearrange("p (a b) t -> p a t b", b=4),
+                in_=out_f32[c // 2][:, :, (c % 2) * CHUNK : (c % 2 + 1) * CHUNK].rearrange("p t (a b) -> p a t b", b=4),
+            )
 
         def quantize_out(c0, c1):
             cols = slice(c0 * CHUNK, c1 * CHUNK)
@@ -240,24 +242,25 @@ def tile_picked_zlayout_gelu_po_kernel(
         quantize_hidden(0)
         quantize_weight(3, 0, 2)
         quantize_weight(3, 2, 4)
-        second_layer(0)
         quantize_hidden(1)
+        second_layer(0)
         quantize_hidden(2)
         first_layer(3)
-        store_rows(0)
         quantize_hidden(3)
-        for c in range(1, CHUNKS):
-            second_layer(c)
-        round_from_bank(1)
-        store_rows(2)
-        round_from_copy(0)
-        round_from_bank(3)
-        store_rows(1)
-        round_from_copy(2)
-        quantize_out(0, 2)
+        second_layer(1)
+        store_rows(0, 0, nc.scalar.copy)
+        store_rows(0, 1, nc.vector.tensor_copy)
+        store_rows(1, 0, nc.scalar.copy)
+        round_from_copy(0, nc.vector.tensor_copy)
+        store_rows(1, 1, nc.vector.tensor_copy)
+        round_from_copy(1, nc.scalar.copy)
+        quantize_out(0, 1)
+        round_from_copy(2, nc.vector.tensor_copy)
+        round_from_copy(3, nc.scalar.copy)
+        quantize_out(1, 2)
         store_codes(0)
-        store_rows(3)
-        quantize_out(2, 4)
+        quantize_out(2, 3)
+        quantize_out(3, 4)
         store_codes(1)
         for q in range(4):
             queue = nc.scalar if q else nc.sync

@@ -129,51 +129,50 @@ def tile_picked_zlayout_gelu_po_kernel(
             )
 
         BANK = 2048
-        first = [psum.tile([P, CHUNK], F32, name="first_%d" % t, offset=t * BANK) for t in range(PACK)]
-        hidden = {c: psum.tile([P, PACK, CHUNK], F32, name="hidden_%d" % c, offset=(3 + c) * BANK) for c in range(1, CHUNKS)}
-        result = [psum.tile([P, 2, 2 * CHUNK], F32, name="result_%d" % b, offset=((b - 1) % 8) * BANK) for b in range(4)]
+        hidden = [psum.tile([P, PACK, CHUNK], F32, name="hidden_%d" % c, offset=c * BANK) for c in range(CHUNKS)]
+        result = [psum.tile([P, 2, 2 * CHUNK], F32, name="result_%d" % b, offset=(4 + b) * BANK) for b in range(4)]
+
+        def order(c):
+            return (1, 2, 0) if c else (1, 0, 2)
 
         def first_layer_pass(i, c, t):
             cols = slice(c * CHUNK, (c + 1) * CHUNK)
             slot = slice(t * P, (t + 1) * P)
             codes = picked_y[c][:] if i == 2 else picked[i][:, cols]
             nc.tensor.matmul_mx(
-                out=hidden[c][:, t, :] if c else first[t][:],
+                out=hidden[c][:, t, :],
                 lhsT=w_codes[i][:, slot].bitcast(FP8X4),
                 lhsT_scale=w_scales[i][:, slot],
                 rhs=codes.bitcast(FP8X4),
                 rhs_scale=planes[:, i * TOKENS + c * CHUNK : i * TOKENS + (c + 1) * CHUNK],
-                start=(i == 1),
-                stop=(i == 2),
+                start=(i == 1 and t == 0),
+                stop=(i == order(c)[2] and t == PACK - 1),
             )
 
-        early = [(0, t) for t in range(PACK)] + [(c, 0) for c in range(1, CHUNKS)]
-        for c, t in early:
-            first_layer_pass(1, c, t)
         for c in range(CHUNKS):
             nc.tensor.matmul_mx(
                 out=result[0][:].rearrange("p t n -> p (t n)"),
-                lhsT=w_codes[0][:, 0:P].bitcast(FP8X4),
-                lhsT_scale=w_scales[0][:, 0:P],
-                rhs=w_codes[1 if c < 2 else 2][:].bitcast(FP8X4),
-                rhs_scale=w_scales[1 if c < 2 else 2][:],
+                lhsT=w_codes[1][:, 0:P].bitcast(FP8X4),
+                lhsT_scale=w_scales[1][:, 0:P],
+                rhs=w_codes[1 if c < 2 else 0][:].bitcast(FP8X4),
+                rhs_scale=w_scales[1 if c < 2 else 0][:],
                 start=True,
                 stop=True,
             )
 
-        for c, t in early:
-            first_layer_pass(0, c, t)
+        for c in range(CHUNKS):
+            for t in range(PACK):
+                first_layer_pass(1, c, t)
 
         deal(nc.scalar.copy, 3, raw4[0][:], 0, 32, 0, 4)
-        h_rows = late.tile([P, PACK, CHUNK], BF16, name="h_rows", offset=13 * KB, align_bytes=64)
-        h_bf = [sb("h_bf_%d" % c, [P, CHUNK, PACK], BF16) for c in range(CHUNKS)]
+        h_bf = [late.tile([P, CHUNK, PACK], BF16, name="h_bf_0", offset=13 * KB, align_bytes=64)]
+        h_bf.extend(sb("h_bf_%d" % c, [P, CHUNK, PACK], BF16) for c in range(1, CHUNKS))
         h_codes = sb("h_codes", [P, TOKENS], U32)
         h_scales = sb("h_scales", [P, TOKENS], U8)
 
         def first_layer(c):
-            first_layer_pass(2, c, 0)
-            for t in range(1, PACK):
-                for i in (1, 0, 2):
+            for i in order(c)[1:]:
+                for t in range(PACK):
                     first_layer_pass(i, c, t)
             nc.scalar.activation(h_bf[c][:], hidden[c][:].rearrange("p t n -> p n t"), GELU)
 
@@ -229,23 +228,18 @@ def tile_picked_zlayout_gelu_po_kernel(
             pair = slice(2 * h * CHUNK, (2 * h + 2) * CHUNK)
             nc.sync.dma_start(out=out_words[:, pair], in_=out_codes[:, pair].bitcast(I32))
 
-        for t in range(PACK):
-            first_layer_pass(2, 0, t)
-            nc.scalar.activation(h_rows[:, t, :], first[t][:], GELU)
+        first_layer(0)
         first_layer(1)
         first_layer(2)
+        first_layer(3)
         deal(nc.vector.tensor_copy, 3, raw4[1][:], 32, 96, 0, 4)
-        nc.vector.tensor_copy(
-            out=h_bf[0][:].rearrange("p (a b) t -> p a t b", b=4), in_=h_rows[:].rearrange("p t (a b) -> p a t b", b=4)
-        )
-        deal(nc.vector.tensor_copy, 3, raw4[2][:], 96, P, 0, 4)
         quantize_hidden(0)
+        deal(nc.vector.tensor_copy, 3, raw4[2][:], 96, P, 0, 4)
+        quantize_hidden(1)
         quantize_weight(3, 0, 2)
         quantize_weight(3, 2, 4)
-        quantize_hidden(1)
         second_layer(0)
         quantize_hidden(2)
-        first_layer(3)
         quantize_hidden(3)
         second_layer(1)
         store_rows(0, 0, nc.scalar.copy)

@@ -130,7 +130,7 @@ def tile_picked_zlayout_gelu_po_kernel(
 
         BANK = 2048
         hidden = [psum.tile([P, PACK, CHUNK], F32, name="hidden_%d" % c, offset=c * BANK) for c in range(CHUNKS)]
-        result = [psum.tile([P, 2, 2 * CHUNK], F32, name="result_%d" % b, offset=(4 + b) * BANK) for b in range(4)]
+        spare = psum.tile([P, TOKENS], F32, name="spare", offset=4 * BANK)
 
         def order(c):
             return (1, 2, 0) if c else (1, 0, 2)
@@ -151,7 +151,7 @@ def tile_picked_zlayout_gelu_po_kernel(
 
         for c in range(CHUNKS):
             nc.tensor.matmul_mx(
-                out=result[0][:].rearrange("p t n -> p (t n)"),
+                out=spare[:],
                 lhsT=w_codes[1][:, 0:P].bitcast(FP8X4),
                 lhsT_scale=w_scales[1][:, 0:P],
                 rhs=w_codes[1 if c < 2 else 0][:].bitcast(FP8X4),
@@ -190,22 +190,23 @@ def tile_picked_zlayout_gelu_po_kernel(
         out_rows = out_0.rearrange("(p t) n -> p t n", t=PACK)
         out_words = out_1[0].rearrange("p n t -> p (n t)").bitcast(I32)
 
-        def second_layer(h):
-            half = slice(2 * h * CHUNK, (2 * h + 2) * CHUNK)
-            for t in range(PACK):
-                slot = slice(t * P, (t + 1) * P)
-                nc.tensor.matmul_mx(
-                    out=result[2 * h + t // 2][:, t % 2, :],
-                    lhsT=w_codes[3][:, slot].bitcast(FP8X4),
-                    lhsT_scale=w_scales[3][:, slot],
-                    rhs=h_codes[:, half].bitcast(FP8X4),
-                    rhs_scale=h_scales[:, half],
-                    start=True,
-                    stop=True,
-                )
+        single = [psum.tile([P, 2 * CHUNK], F32, name="single_%d" % t, offset=(4 + t) * BANK) for t in range(PACK)]
+        double = [psum.tile([P, 2, 2 * CHUNK], F32, name="double_%d" % u, offset=u * BANK) for u in range(2)]
 
-        def store_rows(h, u, copy):
-            copy(out=out_f32[h][:, 2 * u : 2 * u + 2, :], in_=result[2 * h + u][:])
+        def second_pass(h, t):
+            half = slice(2 * h * CHUNK, (2 * h + 2) * CHUNK)
+            slot = slice(t * P, (t + 1) * P)
+            nc.tensor.matmul_mx(
+                out=double[t // 2][:, t % 2, :] if h else single[t][:],
+                lhsT=w_codes[3][:, slot].bitcast(FP8X4),
+                lhsT_scale=w_scales[3][:, slot],
+                rhs=h_codes[:, half].bitcast(FP8X4),
+                rhs_scale=h_scales[:, half],
+                start=True,
+                stop=True,
+            )
+
+        def store_rows(h, u):
             nc.sync.dma_start(
                 out=out_rows[:, 2 * u : 2 * u + 2, 2 * h * CHUNK : (2 * h + 2) * CHUNK], in_=out_f32[h][:, 2 * u : 2 * u + 2, :]
             )
@@ -236,17 +237,23 @@ def tile_picked_zlayout_gelu_po_kernel(
         quantize_hidden(0)
         deal(nc.vector.tensor_copy, 3, raw4[2][:], 96, P, 0, 4)
         quantize_hidden(1)
-        quantize_weight(3, 0, 2)
-        quantize_weight(3, 2, 4)
-        second_layer(0)
+        for t in range(PACK):
+            quantize_weight(3, t, t + 1)
+            second_pass(0, t)
         quantize_hidden(2)
         quantize_hidden(3)
-        second_layer(1)
-        store_rows(0, 0, nc.scalar.copy)
-        store_rows(0, 1, nc.vector.tensor_copy)
-        store_rows(1, 0, nc.scalar.copy)
+        for t in range(PACK):
+            second_pass(1, t)
+        for t in range(PACK):
+            copy = nc.vector.tensor_copy if t == 2 else nc.scalar.copy
+            copy(out=out_f32[0][:, t, :], in_=single[t][:])
+            if t % 2:
+                store_rows(0, t // 2)
+        nc.scalar.copy(out=out_f32[1][:, 0:2, :], in_=double[0][:])
+        store_rows(1, 0)
         round_from_copy(0, nc.vector.tensor_copy)
-        store_rows(1, 1, nc.vector.tensor_copy)
+        nc.vector.tensor_copy(out=out_f32[1][:, 2:4, :], in_=double[1][:])
+        store_rows(1, 1)
         round_from_copy(1, nc.scalar.copy)
         quantize_out(0, 1)
         round_from_copy(2, nc.vector.tensor_copy)

@@ -42,7 +42,7 @@ def tile_picked_zlayout_gelu_po_kernel(
         KB = 1024
         held = late.tile([P, 21 * KB], U8, name="scales_e", offset=0, align_bytes=64)
         table_words = [
-            sb("words_x", [P, columns[0]], I32),
+            late.tile([P, columns[0]], I32, name="words_x", offset=KB, align_bytes=64),
             sb("words_e", [P, columns[1]], I32),
             late.tile([P, columns[2]], I32, name="words_y", offset=9 * KB, align_bytes=64),
         ]
@@ -80,12 +80,12 @@ def tile_picked_zlayout_gelu_po_kernel(
         load_weight(raw[1], w2, 0, WIDTH)
         load_weight(raw[0], w1, 0, WIDTH)
         load_weight(raw[2], w3, 0, WIDTH)
-        load_words(0)
 
         for i in (0, 2, 1):
             nc.vector.tensor_copy(picked_rows[:, i * TOKENS : (i + 1) * TOKENS], table_scales[i].indirect(lists[i][:]))
         for r in range(4):
             nc.sync.dma_start(out=planes[r:P:32, :].bitcast(I32), in_=picked_rows[ROWS + r : P : 4, :].bitcast(I32))
+        load_words(0)
         load_words(2)
         for i in range(3):
             load_weight(raw4[i], w4, cut4[i], cut4[i + 1])
@@ -107,13 +107,11 @@ def tile_picked_zlayout_gelu_po_kernel(
                 in_=grouped[i][:, t0:t1].rearrange("p t m j -> p (t m j)"),
             )
 
-        picked = [sb("picked_" + names[i], [P, TOKENS], U32) for i in range(2)]
+        picked_e = sb("picked_e", [P, TOKENS], U32)
+        picked_x = [sb("picked_x_%d" % h, [P, 2 * CHUNK], U32) for h in range(2)]
         picked_y = [sb("picked_y_%d" % c, [P, CHUNK], U32) for c in range(CHUNKS)]
 
-        def pick_words(i):
-            nc.vector.tensor_copy(picked[i][:], table_words[i][:].bitcast(U32).indirect(lists[i][:]))
-
-        pick_words(1)
+        nc.vector.tensor_copy(picked_e[:], table_words[1][:].bitcast(U32).indirect(lists[1][:]))
         deal(nc.scalar.copy, 1, raw[1][:], 0, P, 0, 4)
         deal(nc.scalar.copy, 0, raw[0][:], 0, P, 0, 2)
         deal(nc.vector.tensor_copy, 0, raw[0][:], 0, P, 2, 4)
@@ -122,7 +120,8 @@ def tile_picked_zlayout_gelu_po_kernel(
         deal(nc.scalar.copy, 2, raw[2][:], 0, P, 0, 2)
         deal(nc.vector.tensor_copy, 2, raw[2][:], 0, P, 2, 4)
         quantize_weight(2)
-        pick_words(0)
+        for h in range(2):
+            nc.vector.tensor_copy(picked_x[h][:], table_words[0][:].bitcast(U32).indirect(lists[0][:, 16 * h : 16 * h + 16]))
         for c in range(CHUNKS):
             nc.vector.tensor_copy(
                 picked_y[c][:], table_words[2][:].bitcast(U32).indirect(lists[2][:, c * CHUNK // 16 : (c + 1) * CHUNK // 16])
@@ -133,12 +132,12 @@ def tile_picked_zlayout_gelu_po_kernel(
         spare = psum.tile([P, TOKENS], F32, name="spare", offset=4 * BANK)
 
         def order(c):
-            return (1, 2, 0) if c else (1, 0, 2)
+            return (1, 2, 0) if c >= 2 else (1, 0, 2)
 
         def first_layer_pass(i, c, t):
             cols = slice(c * CHUNK, (c + 1) * CHUNK)
             slot = slice(t * P, (t + 1) * P)
-            codes = picked_y[c][:] if i == 2 else picked[i][:, cols]
+            codes = (picked_x[c // 2][:, (c % 2) * CHUNK : (c % 2 + 1) * CHUNK], picked_e[:, cols], picked_y[c][:])[i]
             nc.tensor.matmul_mx(
                 out=hidden[c][:, t, :],
                 lhsT=w_codes[i][:, slot].bitcast(FP8X4),
@@ -150,37 +149,37 @@ def tile_picked_zlayout_gelu_po_kernel(
             )
 
         for c in range(CHUNKS):
+            for t in range(PACK):
+                first_layer_pass(1, c, t)
+
+        for c in range(2):
             nc.tensor.matmul_mx(
                 out=spare[:],
-                lhsT=w_codes[1][:, 0:P].bitcast(FP8X4),
-                lhsT_scale=w_scales[1][:, 0:P],
-                rhs=w_codes[1 if c < 2 else 0][:].bitcast(FP8X4),
-                rhs_scale=w_scales[1 if c < 2 else 0][:],
+                lhsT=w_codes[2][:, 0:P].bitcast(FP8X4),
+                lhsT_scale=w_scales[2][:, 0:P],
+                rhs=picked_e[:].bitcast(FP8X4),
+                rhs_scale=planes[:, TOKENS : 2 * TOKENS],
                 start=True,
                 stop=True,
             )
 
-        for c in range(CHUNKS):
-            for t in range(PACK):
-                first_layer_pass(1, c, t)
-
         deal(nc.scalar.copy, 3, raw4[0][:], 0, 32, 0, 4)
-        h_bf = [late.tile([P, CHUNK, PACK], BF16, name="h_bf_0", offset=13 * KB, align_bytes=64)]
-        h_bf.extend(sb("h_bf_%d" % c, [P, CHUNK, PACK], BF16) for c in range(1, CHUNKS))
-        h_codes = sb("h_codes", [P, TOKENS], U32)
+        h_bf = [late.tile([P, 2, CHUNK, PACK], BF16, name="h_bf_0", offset=13 * KB, align_bytes=64), sb("h_bf_1", [P, 2, CHUNK, PACK], BF16)]
+        h_codes = [sb("h_codes_0", [P, 2 * CHUNK], U32), late.tile([P, 2 * CHUNK], U32, name="h_codes_1", offset=19 * KB, align_bytes=64)]
         h_scales = sb("h_scales", [P, TOKENS], U8)
 
         def first_layer(c):
             for i in order(c)[1:]:
                 for t in range(PACK):
                     first_layer_pass(i, c, t)
-            nc.scalar.activation(h_bf[c][:], hidden[c][:].rearrange("p t n -> p n t"), GELU)
+            nc.scalar.activation(h_bf[c // 2][:, c % 2], hidden[c][:].rearrange("p t n -> p n t"), GELU)
 
-        def quantize_hidden(c):
+        def quantize_hidden(c0, c1):
+            lo, hi = c0 % 2, c0 % 2 + c1 - c0
             nc.vector.quantize_mx(
-                out=h_codes[:, c * CHUNK : (c + 1) * CHUNK].bitcast(FP8X4),
-                scales=h_scales[:, c * CHUNK : (c + 1) * CHUNK],
-                in_=h_bf[c][:].rearrange("p n t -> p (n t)"),
+                out=h_codes[c0 // 2][:, lo * CHUNK : hi * CHUNK].bitcast(FP8X4),
+                scales=h_scales[:, c0 * CHUNK : c1 * CHUNK],
+                in_=h_bf[c0 // 2][:, lo:hi].rearrange("p c n t -> p (c n t)"),
             )
 
         out_f32 = [sb("out_f32_%d" % h, [P, PACK, 2 * CHUNK], F32) for h in range(2)]
@@ -200,7 +199,7 @@ def tile_picked_zlayout_gelu_po_kernel(
                 out=double[t // 2][:, t % 2, :] if h else single[t][:],
                 lhsT=w_codes[3][:, slot].bitcast(FP8X4),
                 lhsT_scale=w_scales[3][:, slot],
-                rhs=h_codes[:, half].bitcast(FP8X4),
+                rhs=h_codes[h][:].bitcast(FP8X4),
                 rhs_scale=h_scales[:, half],
                 start=True,
                 stop=True,
@@ -234,14 +233,14 @@ def tile_picked_zlayout_gelu_po_kernel(
         first_layer(2)
         first_layer(3)
         deal(nc.vector.tensor_copy, 3, raw4[1][:], 32, 96, 0, 4)
-        quantize_hidden(0)
+        quantize_hidden(0, 1)
         deal(nc.vector.tensor_copy, 3, raw4[2][:], 96, P, 0, 4)
-        quantize_hidden(1)
+        quantize_hidden(1, 2)
         for t in range(PACK):
             quantize_weight(3, t, t + 1)
             second_pass(0, t)
-        quantize_hidden(2)
-        quantize_hidden(3)
+        quantize_hidden(2, 3)
+        quantize_hidden(3, 4)
         for t in range(PACK):
             second_pass(1, t)
         for t in range(PACK):

@@ -17,7 +17,11 @@ WIDTH = 512
 TOKENS = 512
 CHUNK = 128
 CHUNKS = TOKENS // CHUNK
+HALF = TOKENS // 2
+KB = 1024
+BANK = 2048
 FLOPS = 4 * 2 * 512 * 512 * 512
+X, E, Y, LAST = 0, 1, 2, 3
 
 
 def tile_picked_zlayout_gelu_po_kernel(
@@ -26,244 +30,226 @@ def tile_picked_zlayout_gelu_po_kernel(
     nc = tc.nc
     with ExitStack() as ctx:
         keep = ctx.enter_context(tc.tile_pool(name="keep", bufs=1))
-        late = ctx.enter_context(tc.tile_pool(name="late", bufs=1))
+        shared = ctx.enter_context(tc.tile_pool(name="shared", bufs=1))
         psum = ctx.enter_context(tc.psum_pool(name="psum", bufs=1))
 
         def sb(name, shape, dtype):
             return keep.tile(shape, dtype, name=name, align_bytes=64)
 
+        def at(name, shape, dtype, offset):
+            return shared.tile(shape, dtype, name=name, offset=offset, align_bytes=64)
+
         names = ("x", "e", "y")
         words_in = (x_words, e_words, y_words)
         scales_in = (x_scales, e_scales, y_scales)
         lists_in = (offs, tok, row)
+        weights_in = (w1, w2, w3)
         columns = [w.shape[2] for w in words_in]
 
         lists = [sb("list_" + n, [P, TOKENS // 16], U16) for n in names]
-        KB = 1024
-        held = late.tile([P, 21 * KB], U8, name="scales_e", offset=0, align_bytes=64)
-        table_words = [
-            late.tile([P, columns[0]], I32, name="words_x", offset=KB, align_bytes=64),
-            sb("words_e", [P, columns[1]], I32),
-            late.tile([P, columns[2]], I32, name="words_y", offset=9 * KB, align_bytes=64),
+        table_scales = [
+            at("scales_x", [P, columns[X]], U8, 8 * KB),
+            at("scales_e", [P, columns[E]], U8, 10 * KB),
+            at("scales_y", [P, columns[Y]], U8, 11 * KB),
         ]
-        table_scales = [sb("scales_x", [P, columns[0]], U8)[:], held[:, 0 : columns[1]], sb("scales_y", [P, columns[2]], U8)[:]]
+        table_words = [
+            at("words_x", [P, columns[X]], I32, 12 * KB),
+            at("words_e", [P, columns[E]], I32, 12 * KB),
+            at("words_y", [P, columns[Y]], I32, 8 * KB),
+        ]
+        raw = [sb("raw_x", [P, PACK, WIDTH], F32), at("raw_e", [P, PACK, WIDTH], F32, 0), sb("raw_y", [P, PACK, WIDTH], F32)]
+        cuts = (0, 128, 384, 512)
+        raw_last = [at("raw_last_%d" % u, [P, PACK, cuts[u + 1] - cuts[u]], F32, 16 * cuts[u]) for u in range(3)]
         picked_rows = sb("picked_rows", [P, 3 * TOKENS], U8)
         planes = sb("planes", [P, 3 * TOKENS], U8)
-        raw = [sb("raw_%d" % i, [P, PACK, WIDTH], F32) for i in range(3)]
-        cut4 = (0, 128, 384, 512)
-        raw4 = [
-            late.tile([P, PACK, cut4[i + 1] - cut4[i]], F32, name="raw4_%d" % i, offset=13 * KB + 16 * cut4[i], align_bytes=64)
-            for i in range(3)
-        ]
         warm_in = sb("warm_in", [P, 8], F32)
         warm_out = sb("warm_out", [P, 8], F32)
 
         ROWS = P - 16
         nc.vector.memset(warm_in[:], 0.0)
-        nc.vector.memset(table_scales[0][0:ROWS, :].bitcast(I32), 0)
-        nc.vector.memset(table_scales[2][0:ROWS, :].bitcast(I32), 0)
-        nc.vector.memset(table_scales[1][0:ROWS, :].bitcast(I32), 0)
+        for i in (X, Y, E):
+            nc.vector.memset(table_scales[i][0:ROWS, :].bitcast(I32), 0)
         nc.vector.memset(planes[:].bitcast(I32), 0)
 
-        def load_weight(dst, w, c0, c1):
-            nc.sync.dma_start(out=dst[:], in_=w.rearrange("(p j) c -> p j c", j=PACK)[:, :, c0:c1])
+        def load_weight(i):
+            nc.sync.dma_start(out=raw[i][:], in_=weights_in[i].rearrange("(p j) c -> p j c", j=PACK))
 
         def load_words(i):
             nc.sync.dma_start(out=table_words[i][:], in_=words_in[i][0].rearrange("p n t -> p (n t)").bitcast(I32))
 
-        load_words(1)
-        for i in (0, 2, 1):
+        load_words(E)
+        for i in (X, Y, E):
             nc.sync.dma_start(lists[i][:], lists_in[i])
-        for i in (0, 2, 1):
+        for i in (X, Y, E):
             nc.scalar.dma_start(out=table_scales[i][ROWS:P, :].bitcast(I32), in_=scales_in[i][0].bitcast(I32))
         nc.scalar.activation(warm_out[:], warm_in[:], GELU)
-        load_weight(raw[1], w2, 0, WIDTH)
-        load_weight(raw[0], w1, 0, WIDTH)
-        load_weight(raw[2], w3, 0, WIDTH)
+        for i in (E, Y, X):
+            load_weight(i)
 
-        for i in (0, 2, 1):
-            nc.vector.tensor_copy(picked_rows[:, i * TOKENS : (i + 1) * TOKENS], table_scales[i].indirect(lists[i][:]))
+        for i in (X, Y, E):
+            nc.vector.tensor_copy(picked_rows[:, i * TOKENS : (i + 1) * TOKENS], table_scales[i][:].indirect(lists[i][:]))
         for r in range(4):
             nc.sync.dma_start(out=planes[r:P:32, :].bitcast(I32), in_=picked_rows[ROWS + r : P : 4, :].bitcast(I32))
-        load_words(0)
-        load_words(2)
-        for i in range(3):
-            load_weight(raw4[i], w4, cut4[i], cut4[i + 1])
+        load_words(Y)
 
-        grouped = [sb("grouped_%d" % i, [P, PACK, P, PACK], BF16) for i in range(4)]
+        picked = [
+            [sb("picked_x_%d" % c, [P, CHUNK], U32) for c in range(CHUNKS)],
+            [sb("picked_e", [P, TOKENS], U32)],
+            [sb("picked_y_%d" % h, [P, HALF], U32) for h in range(2)],
+        ]
+
+        def gather_words(i):
+            step = TOKENS // 16 // len(picked[i])
+            for n, tile in enumerate(picked[i]):
+                nc.vector.tensor_copy(tile[:], table_words[i][:].bitcast(U32).indirect(lists[i][:, n * step : (n + 1) * step]))
+
+        gather_words(E)
+        load_words(X)
+
+        grouped = [sb("grouped_" + n, [P, PACK, P, PACK], BF16) for n in names]
+        last_grouped = sb("last_grouped", [P, PACK, P, PACK], BF16)
         w_codes = [sb("w_codes_%d" % i, [P, WIDTH], U32) for i in range(4)]
         w_scales = [sb("w_scales_%d" % i, [P, WIDTH], U8) for i in range(4)]
 
-        def deal(copy, i, src, m0, m1, t0, t1):
+        def deal(copy, dst, src, t0, t1):
             copy(
-                out=grouped[i][:, t0:t1, m0:m1, :].rearrange("p t m j -> p m j t"),
+                out=dst[:, t0:t1].rearrange("p t m j -> p m j t"),
                 in_=src.rearrange("p j (m t) -> p m j t", t=PACK)[:, :, :, t0:t1],
             )
 
-        def quantize_weight(i, t0=0, t1=PACK):
-            nc.vector.quantize_mx(
-                out=w_codes[i][:, t0 * P : t1 * P].bitcast(FP8X4),
-                scales=w_scales[i][:, t0 * P : t1 * P],
-                in_=grouped[i][:, t0:t1].rearrange("p t m j -> p (t m j)"),
-            )
+        def deal_last(u, copy):
+            deal(copy, last_grouped[:, :, cuts[u] // PACK : cuts[u + 1] // PACK, :], raw_last[u][:], 0, PACK)
 
-        picked_e = sb("picked_e", [P, TOKENS], U32)
-        picked_x = [sb("picked_x_%d" % h, [P, 2 * CHUNK], U32) for h in range(2)]
-        picked_y = [sb("picked_y_%d" % c, [P, CHUNK], U32) for c in range(CHUNKS)]
+        def quantize(codes, scales, values):
+            nc.vector.quantize_mx(out=codes.bitcast(FP8X4), scales=scales, in_=values)
 
-        nc.vector.tensor_copy(picked_e[:], table_words[1][:].bitcast(U32).indirect(lists[1][:]))
-        deal(nc.scalar.copy, 1, raw[1][:], 0, P, 0, 4)
-        deal(nc.scalar.copy, 0, raw[0][:], 0, P, 0, 2)
-        deal(nc.vector.tensor_copy, 0, raw[0][:], 0, P, 2, 4)
-        quantize_weight(1)
-        quantize_weight(0)
-        deal(nc.scalar.copy, 2, raw[2][:], 0, P, 0, 2)
-        deal(nc.vector.tensor_copy, 2, raw[2][:], 0, P, 2, 4)
-        quantize_weight(2)
-        for h in range(2):
-            nc.vector.tensor_copy(picked_x[h][:], table_words[0][:].bitcast(U32).indirect(lists[0][:, 16 * h : 16 * h + 16]))
-        for c in range(CHUNKS):
-            nc.vector.tensor_copy(
-                picked_y[c][:], table_words[2][:].bitcast(U32).indirect(lists[2][:, c * CHUNK // 16 : (c + 1) * CHUNK // 16])
-            )
+        def quantize_weight(i):
+            quantize(w_codes[i][:], w_scales[i][:], grouped[i][:].rearrange("p t m j -> p (t m j)"))
 
-        BANK = 2048
+        deal(nc.scalar.copy, grouped[E][:], raw[E][:], 0, 4)
+        for u in range(3):
+            nc.sync.dma_start(out=raw_last[u][:], in_=w4.rearrange("(p j) c -> p j c", j=PACK)[:, :, cuts[u] : cuts[u + 1]])
+        deal(nc.scalar.copy, grouped[Y][:], raw[Y][:], 0, 2)
+        deal(nc.vector.tensor_copy, grouped[Y][:], raw[Y][:], 2, 4)
+        quantize_weight(E)
+        quantize_weight(Y)
+        deal(nc.scalar.copy, grouped[X][:], raw[X][:], 0, 2)
+        deal(nc.vector.tensor_copy, grouped[X][:], raw[X][:], 2, 4)
+        gather_words(Y)
+        quantize_weight(X)
+        gather_words(X)
+
         hidden = [psum.tile([P, PACK, CHUNK], F32, name="hidden_%d" % c, offset=c * BANK) for c in range(CHUNKS)]
-        spare = psum.tile([P, TOKENS], F32, name="spare", offset=4 * BANK)
 
         def order(c):
-            return (1, 2, 0) if c >= 2 else (1, 0, 2)
+            return (E, Y, X) if c < 2 else (E, X, Y)
 
-        def first_layer_pass(i, c, t):
-            cols = slice(c * CHUNK, (c + 1) * CHUNK)
-            slot = slice(t * P, (t + 1) * P)
-            codes = (picked_x[c // 2][:, (c % 2) * CHUNK : (c % 2 + 1) * CHUNK], picked_e[:, cols], picked_y[c][:])[i]
-            nc.tensor.matmul_mx(
-                out=hidden[c][:, t, :],
-                lhsT=w_codes[i][:, slot].bitcast(FP8X4),
-                lhsT_scale=w_scales[i][:, slot],
-                rhs=codes.bitcast(FP8X4),
-                rhs_scale=planes[:, i * TOKENS + c * CHUNK : i * TOKENS + (c + 1) * CHUNK],
-                start=(i == 1 and t == 0),
-                stop=(i == order(c)[2] and t == PACK - 1),
-            )
+        def first_layer_passes(i, c):
+            per_tile = CHUNKS // len(picked[i])
+            codes = picked[i][c // per_tile][:, (c % per_tile) * CHUNK : (c % per_tile + 1) * CHUNK]
+            for t in range(PACK):
+                slot = slice(t * P, (t + 1) * P)
+                nc.tensor.matmul_mx(
+                    out=hidden[c][:, t, :],
+                    lhsT=w_codes[i][:, slot].bitcast(FP8X4),
+                    lhsT_scale=w_scales[i][:, slot],
+                    rhs=codes.bitcast(FP8X4),
+                    rhs_scale=planes[:, i * TOKENS + c * CHUNK : i * TOKENS + (c + 1) * CHUNK],
+                    start=(i == E and t == 0),
+                    stop=(i == order(c)[2] and t == PACK - 1),
+                )
+
+        h_bf = sb("h_bf", [P, CHUNKS, CHUNK, PACK], BF16)
+        h_codes = [sb("h_codes_0", [P, HALF], U32), at("h_codes_1", [P, HALF], U32, 16 * cuts[2])]
+        h_scales = [sb("h_scales_%d" % h, [P, HALF], U8) for h in range(2)]
 
         for c in range(CHUNKS):
-            for t in range(PACK):
-                first_layer_pass(1, c, t)
-
-        for c in range(2):
-            nc.tensor.matmul_mx(
-                out=spare[:],
-                lhsT=w_codes[2][:, 0:P].bitcast(FP8X4),
-                lhsT_scale=w_scales[2][:, 0:P],
-                rhs=picked_e[:].bitcast(FP8X4),
-                rhs_scale=planes[:, TOKENS : 2 * TOKENS],
-                start=True,
-                stop=True,
-            )
-
-        deal(nc.scalar.copy, 3, raw4[0][:], 0, 32, 0, 4)
-        h_bf = [late.tile([P, 2, CHUNK, PACK], BF16, name="h_bf_0", offset=13 * KB, align_bytes=64), sb("h_bf_1", [P, 2, CHUNK, PACK], BF16)]
-        h_codes = [sb("h_codes_0", [P, 2 * CHUNK], U32), late.tile([P, 2 * CHUNK], U32, name="h_codes_1", offset=19 * KB, align_bytes=64)]
-        h_scales = sb("h_scales", [P, TOKENS], U8)
-
-        def first_layer(c):
+            first_layer_passes(E, c)
+        deal_last(0, nc.scalar.copy)
+        for c in range(CHUNKS):
             for i in order(c)[1:]:
-                for t in range(PACK):
-                    first_layer_pass(i, c, t)
-            nc.scalar.activation(h_bf[c // 2][:, c % 2], hidden[c][:].rearrange("p t n -> p n t"), GELU)
+                first_layer_passes(i, c)
+            nc.scalar.activation(h_bf[:, c], hidden[c][:].rearrange("p t n -> p n t"), GELU)
 
-        def quantize_hidden(c0, c1):
-            lo, hi = c0 % 2, c0 % 2 + c1 - c0
-            nc.vector.quantize_mx(
-                out=h_codes[c0 // 2][:, lo * CHUNK : hi * CHUNK].bitcast(FP8X4),
-                scales=h_scales[:, c0 * CHUNK : c1 * CHUNK],
-                in_=h_bf[c0 // 2][:, lo:hi].rearrange("p c n t -> p (c n t)"),
-            )
+        def quantize_hidden(c):
+            cols = slice((c % 2) * CHUNK, (c % 2 + 1) * CHUNK)
+            quantize(h_codes[c // 2][:, cols], h_scales[c // 2][:, cols], h_bf[:, c].rearrange("p n t -> p (n t)"))
 
-        out_f32 = [sb("out_f32_%d" % h, [P, PACK, 2 * CHUNK], F32) for h in range(2)]
-        out_bf = [sb("out_bf_%d" % h, [P, 2, CHUNK, PACK], BF16) for h in range(2)]
+        def quantize_last(t):
+            slot = slice(t * P, (t + 1) * P)
+            quantize(w_codes[LAST][:, slot], w_scales[LAST][:, slot], last_grouped[:, t].rearrange("p m j -> p (m j)"))
+
+        out_f32 = [sb("out_f32_%d" % h, [P, PACK, HALF], F32) for h in range(2)]
+        out_bf = [sb("out_bf_%d" % c, [P, CHUNK, PACK], BF16) for c in range(CHUNKS)]
         out_codes = sb("out_codes", [P, TOKENS], U32)
         out_scales = sb("out_scales", [P, TOKENS], U8)
         out_rows = out_0.rearrange("(p t) n -> p t n", t=PACK)
         out_words = out_1[0].rearrange("p n t -> p (n t)").bitcast(I32)
 
-        single = [psum.tile([P, 2 * CHUNK], F32, name="single_%d" % t, offset=(4 + t) * BANK) for t in range(PACK)]
-        double = [psum.tile([P, 2, 2 * CHUNK], F32, name="double_%d" % u, offset=u * BANK) for u in range(2)]
+        single = [psum.tile([P, HALF], F32, name="single_%d" % t, offset=(4 + t) * BANK) for t in range(PACK)]
+        pair = [psum.tile([P, 2, HALF], F32, name="pair_%d" % u, offset=u * BANK) for u in range(2)]
 
-        def second_pass(h, t):
-            half = slice(2 * h * CHUNK, (2 * h + 2) * CHUNK)
+        def second_pass(dst, h, t):
             slot = slice(t * P, (t + 1) * P)
             nc.tensor.matmul_mx(
-                out=double[t // 2][:, t % 2, :] if h else single[t][:],
-                lhsT=w_codes[3][:, slot].bitcast(FP8X4),
-                lhsT_scale=w_scales[3][:, slot],
+                out=dst,
+                lhsT=w_codes[LAST][:, slot].bitcast(FP8X4),
+                lhsT_scale=w_scales[LAST][:, slot],
                 rhs=h_codes[h][:].bitcast(FP8X4),
-                rhs_scale=h_scales[:, half],
+                rhs_scale=h_scales[h][:],
                 start=True,
                 stop=True,
             )
 
-        def store_rows(h, u):
-            nc.sync.dma_start(
-                out=out_rows[:, 2 * u : 2 * u + 2, 2 * h * CHUNK : (2 * h + 2) * CHUNK], in_=out_f32[h][:, 2 * u : 2 * u + 2, :]
-            )
+        def tokens(h):
+            return slice(h * HALF, (h + 1) * HALF)
 
-        def round_from_copy(c, copy):
+        def store_rows(h, t0, t1):
+            nc.sync.dma_start(out=out_rows[:, t0:t1, tokens(h)], in_=out_f32[h][:, t0:t1, :])
+
+        def store_codes(h):
+            nc.sync.dma_start(out=out_words[:, tokens(h)], in_=out_codes[:, tokens(h)].bitcast(I32))
+
+        def round_out(c, copy):
             copy(
-                out=out_bf[c // 2][:, c % 2].rearrange("p (a b) t -> p a t b", b=4),
+                out=out_bf[c][:].rearrange("p (a b) t -> p a t b", b=4),
                 in_=out_f32[c // 2][:, :, (c % 2) * CHUNK : (c % 2 + 1) * CHUNK].rearrange("p t (a b) -> p a t b", b=4),
             )
 
-        def quantize_out(c0, c1):
-            cols = slice(c0 * CHUNK, c1 * CHUNK)
-            nc.vector.quantize_mx(
-                out=out_codes[:, cols].bitcast(FP8X4),
-                scales=out_scales[:, cols],
-                in_=out_bf[c0 // 2][:, c0 % 2 : c0 % 2 + c1 - c0].rearrange("p c n t -> p (c n t)"),
-            )
+        def quantize_out(c):
+            cols = slice(c * CHUNK, (c + 1) * CHUNK)
+            quantize(out_codes[:, cols], out_scales[:, cols], out_bf[c][:].rearrange("p n t -> p (n t)"))
 
-        def store_codes(h):
-            pair = slice(2 * h * CHUNK, (2 * h + 2) * CHUNK)
-            nc.sync.dma_start(out=out_words[:, pair], in_=out_codes[:, pair].bitcast(I32))
-
-        first_layer(0)
-        first_layer(1)
-        first_layer(2)
-        first_layer(3)
-        deal(nc.vector.tensor_copy, 3, raw4[1][:], 32, 96, 0, 4)
-        quantize_hidden(0, 1)
-        deal(nc.vector.tensor_copy, 3, raw4[2][:], 96, P, 0, 4)
-        quantize_hidden(1, 2)
+        deal_last(1, nc.vector.tensor_copy)
+        quantize_hidden(0)
+        deal_last(2, nc.vector.tensor_copy)
+        quantize_hidden(1)
         for t in range(PACK):
-            quantize_weight(3, t, t + 1)
-            second_pass(0, t)
-        quantize_hidden(2, 3)
-        quantize_hidden(3, 4)
+            quantize_last(t)
+            second_pass(single[t][:], 0, t)
+        quantize_hidden(2)
+        quantize_hidden(3)
         for t in range(PACK):
-            second_pass(1, t)
+            second_pass(pair[t // 2][:, t % 2, :], 1, t)
         for t in range(PACK):
             copy = nc.vector.tensor_copy if t == 2 else nc.scalar.copy
             copy(out=out_f32[0][:, t, :], in_=single[t][:])
             if t % 2:
-                store_rows(0, t // 2)
-        nc.scalar.copy(out=out_f32[1][:, 0:2, :], in_=double[0][:])
-        store_rows(1, 0)
-        round_from_copy(0, nc.vector.tensor_copy)
-        nc.vector.tensor_copy(out=out_f32[1][:, 2:4, :], in_=double[1][:])
-        store_rows(1, 1)
-        round_from_copy(1, nc.scalar.copy)
-        quantize_out(0, 1)
-        round_from_copy(2, nc.vector.tensor_copy)
-        round_from_copy(3, nc.scalar.copy)
-        quantize_out(1, 2)
+                store_rows(0, t - 1, t + 1)
+        nc.scalar.copy(out=out_f32[1][:, 0:2, :], in_=pair[0][:])
+        store_rows(1, 0, 2)
+        round_out(0, nc.vector.tensor_copy)
+        nc.vector.tensor_copy(out=out_f32[1][:, 2:4, :], in_=pair[1][:])
+        store_rows(1, 2, 4)
+        round_out(1, nc.scalar.copy)
+        quantize_out(0)
+        round_out(2, nc.vector.tensor_copy)
+        round_out(3, nc.scalar.copy)
+        quantize_out(1)
         store_codes(0)
-        quantize_out(2, 3)
-        quantize_out(3, 4)
+        quantize_out(2)
+        quantize_out(3)
         store_codes(1)
         for q in range(4):
             queue = nc.scalar if q else nc.sync
-            queue.dma_start(
-                out=out_2[0, q:16:4, :].bitcast(I32), in_=out_scales[q:P:32, :].bitcast(I32)
-            )
+            queue.dma_start(out=out_2[0, q:16:4, :].bitcast(I32), in_=out_scales[q:P:32, :].bitcast(I32))

@@ -60,16 +60,23 @@ def tile_picked_zlayout_gelu_po_kernel(
         raw = [sb("raw_x", [P, PACK, WIDTH], F32), at("raw_e", [P, PACK, WIDTH], F32, 0), sb("raw_y", [P, PACK, WIDTH], F32)]
         cuts = (0, 128, 384, 512)
         raw_last = [at("raw_last_%d" % u, [P, PACK, cuts[u + 1] - cuts[u]], F32, 16 * cuts[u]) for u in range(3)]
-        picked_rows = sb("picked_rows", [P, 3 * TOKENS], U8)
-        planes = sb("planes", [P, 3 * TOKENS], U8)
+        place = {X: 0, E: 0, Y: TOKENS}
+        first_row = {X: 112, E: 48, Y: 48}
+        plane_row = {X: 0, E: 4, Y: 4}
+        picked_rows = {X: sb("picked_rows_x", [P, TOKENS], U8)}
+        planes = {X: sb("planes_x", [P, TOKENS], U8)}
+        picked_rows[E] = picked_rows[Y] = sb("picked_rows_ey", [P, 2 * TOKENS], U8)
+        planes[E] = planes[Y] = sb("planes_ey", [P, 2 * TOKENS], U8)
         warm_in = sb("warm_in", [P, 8], F32)
         warm_out = sb("warm_out", [P, 8], F32)
 
-        ROWS = P - 16
         nc.vector.memset(warm_in[:], 0.0)
         for i in (X, Y, E):
-            nc.vector.memset(table_scales[i][0:ROWS, :].bitcast(I32), 0)
-        nc.vector.memset(planes[:].bitcast(I32), 0)
+            nc.vector.memset(table_scales[i][0 : first_row[i], :].bitcast(I32), 0)
+            if first_row[i] + 16 < P:
+                nc.vector.memset(table_scales[i][first_row[i] + 16 : P, :].bitcast(I32), 0)
+        for i in (X, E):
+            nc.vector.memset(planes[i][:].bitcast(I32), 0)
 
         def load_weight(i):
             nc.sync.dma_start(out=raw[i][:], in_=weights_in[i].rearrange("(p j) c -> p j c", j=PACK))
@@ -81,15 +88,19 @@ def tile_picked_zlayout_gelu_po_kernel(
         for i in (X, Y, E):
             nc.sync.dma_start(lists[i][:], lists_in[i])
         for i in (X, Y, E):
-            nc.scalar.dma_start(out=table_scales[i][ROWS:P, :].bitcast(I32), in_=scales_in[i][0].bitcast(I32))
+            nc.scalar.dma_start(out=table_scales[i][first_row[i] : first_row[i] + 16, :].bitcast(I32), in_=scales_in[i][0].bitcast(I32))
         nc.scalar.activation(warm_out[:], warm_in[:], GELU)
         for i in (E, Y, X):
             load_weight(i)
 
         for i in (X, Y, E):
-            nc.vector.tensor_copy(picked_rows[:, i * TOKENS : (i + 1) * TOKENS], table_scales[i][:].indirect(lists[i][:]))
-        for r in range(4):
-            nc.sync.dma_start(out=planes[r:P:32, :].bitcast(I32), in_=picked_rows[ROWS + r : P : 4, :].bitcast(I32))
+            nc.vector.tensor_copy(picked_rows[i][:, place[i] : place[i] + TOKENS], table_scales[i][:].indirect(lists[i][:]))
+        for i, queue in ((X, nc.gpsimd), (E, nc.sync)):
+            for r in range(4):
+                queue.dma_start(
+                    out=planes[i][plane_row[i] + r : P : 32, :].bitcast(I32),
+                    in_=picked_rows[i][first_row[i] + r : first_row[i] + 16 : 4, :].bitcast(I32),
+                )
         load_words(Y)
 
         picked = [
@@ -154,7 +165,7 @@ def tile_picked_zlayout_gelu_po_kernel(
                     lhsT=w_codes[i][:, slot].bitcast(FP8X4),
                     lhsT_scale=w_scales[i][:, slot],
                     rhs=codes.bitcast(FP8X4),
-                    rhs_scale=planes[:, i * TOKENS + c * CHUNK : i * TOKENS + (c + 1) * CHUNK],
+                    rhs_scale=planes[i][plane_row[i] : P, place[i] + c * CHUNK : place[i] + (c + 1) * CHUNK],
                     start=(i == E and t == 0),
                     stop=(i == order(c)[2] and t == PACK - 1),
                 )

@@ -190,7 +190,8 @@ def tile_picked_zlayout_gelu_po_kernel(
             slot = slice(t * P, (t + 1) * P)
             quantize(w_codes[LAST][:, slot], w_scales[LAST][:, slot], last_grouped[:, t].rearrange("p m j -> p (m j)"))
 
-        out_f32 = [sb("out_f32_%d" % h, [P, PACK, HALF], F32) for h in range(2)]
+        out_all = sb("out_all", [P, PACK, TOKENS], F32)
+        out_f32 = [out_all[:, :, h * HALF : (h + 1) * HALF] for h in range(2)]
         out_bf = [sb("out_bf_%d" % c, [P, CHUNK, PACK], BF16) for c in range(CHUNKS)]
         out_codes = sb("out_codes", [P, TOKENS], U32)
         out_scales = sb("out_scales", [P, TOKENS], U8)
@@ -245,13 +246,16 @@ def tile_picked_zlayout_gelu_po_kernel(
         for t in range(PACK):
             copy = nc.vector.tensor_copy if t == 2 else nc.scalar.copy
             copy(out=out_f32[0][:, t, :], in_=single[t][:])
-            if t % 2:
-                store_rows(0, t - 1, t + 1)
+            if t == 0:
+                store_rows(0, 0, 1)
+            if t == 2:
+                store_rows(0, 1, 3)
         nc.scalar.copy(out=out_f32[1][:, 0:2, :], in_=pair[0][:])
         store_rows(1, 0, 2)
         round_out(0, nc.vector.tensor_copy)
         nc.vector.tensor_copy(out=out_f32[1][:, 2:4, :], in_=pair[1][:])
-        store_rows(1, 2, 4)
+        rest = slice(2 * TOKENS + HALF, PACK * TOKENS)
+        nc.sync.dma_start(out=out_rows.rearrange("p t n -> p (t n)")[:, rest], in_=out_all[:].rearrange("p t n -> p (t n)")[:, rest])
         round_out(1, nc.scalar.copy)
         quantize_out(0)
         round_out(2, nc.vector.tensor_copy)

@@ -252,16 +252,16 @@ def tile_picked_zlayout_gelu_po_kernel(
                 store_rows(0, 1, 3)
         nc.scalar.copy(out=out_f32[1][:, 0:2, :], in_=pair[0][:])
         store_rows(1, 0, 2)
-        round_out(0, nc.vector.tensor_copy)
-        nc.vector.tensor_copy(out=out_f32[1][:, 2:4, :], in_=pair[1][:])
+        nc.scalar.copy(out=out_f32[1][:, 2:4, :], in_=pair[1][:])
         rest = slice(2 * TOKENS + HALF, PACK * TOKENS)
         nc.sync.dma_start(out=out_rows.rearrange("p t n -> p (t n)")[:, rest], in_=out_all[:].rearrange("p t n -> p (t n)")[:, rest])
-        round_out(1, nc.scalar.copy)
+        round_out(0, nc.vector.tensor_copy)
+        round_out(1, nc.vector.tensor_copy)
         quantize_out(0)
-        round_out(2, nc.vector.tensor_copy)
-        round_out(3, nc.scalar.copy)
         quantize_out(1)
         store_codes(0)
+        round_out(2, nc.vector.tensor_copy)
+        round_out(3, nc.scalar.copy)
         quantize_out(2)
         quantize_out(3)
         store_codes(1)

@@ -22,6 +22,8 @@ KB = 1024
 BANK = 2048
 FLOPS = 4 * 2 * 512 * 512 * 512
 X, E, Y, LAST = 0, 1, 2, 3
+CUTS = (0, 128, 384, 512)
+PIECES = len(CUTS) - 1
 
 
 def tile_picked_zlayout_gelu_po_kernel(
@@ -49,17 +51,16 @@ def tile_picked_zlayout_gelu_po_kernel(
         lists = [sb("list_" + n, [P, TOKENS // 16], U16) for n in names]
         table_scales = [
             at("scales_x", [P, columns[X]], U8, 8 * KB),
-            at("scales_e", [P, columns[E]], U8, 10 * KB),
-            at("scales_y", [P, columns[Y]], U8, 11 * KB),
+            at("scales_e", [P, columns[E]], U8, 16 * KB),
+            at("scales_y", [P, columns[Y]], U8, 17 * KB),
         ]
         table_words = [
-            at("words_x", [P, columns[X]], I32, 12 * KB),
-            at("words_e", [P, columns[E]], I32, 12 * KB),
-            at("words_y", [P, columns[Y]], I32, 8 * KB),
+            at("words_x", [P, columns[X]], I32, 20 * KB),
+            at("words_e", [P, columns[E]], I32, 20 * KB),
+            at("words_y", [P, columns[Y]], I32, 16 * KB),
         ]
-        raw = [sb("raw_x", [P, PACK, WIDTH], F32), at("raw_e", [P, PACK, WIDTH], F32, 0), sb("raw_y", [P, PACK, WIDTH], F32)]
-        cuts = (0, 128, 384, 512)
-        raw_last = [at("raw_last_%d" % u, [P, PACK, cuts[u + 1] - cuts[u]], F32, 16 * cuts[u]) for u in range(3)]
+        raw = [at("raw_x", [P, PACK, WIDTH], F32, 8 * KB), at("raw_e", [P, PACK, WIDTH], F32, 0), sb("raw_y", [P, PACK, WIDTH], F32)]
+        raw_last = [at("raw_last_%d" % u, [P, PACK, CUTS[u + 1] - CUTS[u]], F32, 16 * CUTS[u]) for u in range(PIECES)]
         place = {X: 0, E: 0, Y: TOKENS}
         first_row = {X: 112, E: 48, Y: 48}
         plane_row = {X: 0, E: 4, Y: 4}
@@ -67,6 +68,7 @@ def tile_picked_zlayout_gelu_po_kernel(
         planes = {X: sb("planes_x", [P, TOKENS], U8)}
         picked_rows[E] = picked_rows[Y] = sb("picked_rows_ey", [P, 2 * TOKENS], U8)
         planes[E] = planes[Y] = sb("planes_ey", [P, 2 * TOKENS], U8)
+        moves = (X, E)
         warm_in = sb("warm_in", [P, 8], F32)
         warm_out = sb("warm_out", [P, 8], F32)
 
@@ -75,11 +77,11 @@ def tile_picked_zlayout_gelu_po_kernel(
             nc.vector.memset(table_scales[i][0 : first_row[i], :].bitcast(I32), 0)
             if first_row[i] + 16 < P:
                 nc.vector.memset(table_scales[i][first_row[i] + 16 : P, :].bitcast(I32), 0)
-        for i in (X, E):
+        for i in moves:
             nc.vector.memset(planes[i][:].bitcast(I32), 0)
 
         def load_weight(i):
-            nc.sync.dma_start(out=raw[i][:], in_=weights_in[i].rearrange("(p j) c -> p j c", j=PACK))
+            nc.sync.dma_start(out=raw[i][:, :, 0:WIDTH], in_=weights_in[i].rearrange("(p j) c -> p j c", j=PACK))
 
         def load_words(i):
             nc.sync.dma_start(out=table_words[i][:], in_=words_in[i][0].rearrange("p n t -> p (n t)").bitcast(I32))
@@ -90,17 +92,22 @@ def tile_picked_zlayout_gelu_po_kernel(
         for i in (X, Y, E):
             nc.scalar.dma_start(out=table_scales[i][first_row[i] : first_row[i] + 16, :].bitcast(I32), in_=scales_in[i][0].bitcast(I32))
         nc.scalar.activation(warm_out[:], warm_in[:], GELU)
-        for i in (E, Y, X):
+        for i in (E, Y):
             load_weight(i)
 
         for i in (X, Y, E):
             nc.vector.tensor_copy(picked_rows[i][:, place[i] : place[i] + TOKENS], table_scales[i][:].indirect(lists[i][:]))
-        for i, queue in ((X, nc.gpsimd), (E, nc.sync)):
+
+        def move_scale_rows(i):
             for r in range(4):
-                queue.dma_start(
+                nc.sync.dma_start(
                     out=planes[i][plane_row[i] + r : P : 32, :].bitcast(I32),
                     in_=picked_rows[i][first_row[i] + r : first_row[i] + 16 : 4, :].bitcast(I32),
                 )
+
+        move_scale_rows(X)
+        load_weight(X)
+        move_scale_rows(E)
         load_words(Y)
 
         picked = [
@@ -128,8 +135,9 @@ def tile_picked_zlayout_gelu_po_kernel(
                 in_=src.rearrange("p j (m t) -> p m j t", t=PACK)[:, :, :, t0:t1],
             )
 
-        def deal_last(u, copy):
-            deal(copy, last_grouped[:, :, cuts[u] // PACK : cuts[u + 1] // PACK, :], raw_last[u][:], 0, PACK)
+        def deal_last(u, copy, c0=0, c1=None):
+            c1 = CUTS[u + 1] - CUTS[u] if c1 is None else c1
+            deal(copy, last_grouped[:, :, (CUTS[u] + c0) // PACK : (CUTS[u] + c1) // PACK, :], raw_last[u][:, :, c0:c1], 0, PACK)
 
         def quantize(codes, scales, values):
             nc.vector.quantize_mx(out=codes.bitcast(FP8X4), scales=scales, in_=values)
@@ -137,15 +145,15 @@ def tile_picked_zlayout_gelu_po_kernel(
         def quantize_weight(i):
             quantize(w_codes[i][:], w_scales[i][:], grouped[i][:].rearrange("p t m j -> p (t m j)"))
 
-        deal(nc.scalar.copy, grouped[E][:], raw[E][:], 0, 4)
-        for u in range(3):
-            nc.sync.dma_start(out=raw_last[u][:], in_=w4.rearrange("(p j) c -> p j c", j=PACK)[:, :, cuts[u] : cuts[u + 1]])
-        deal(nc.scalar.copy, grouped[Y][:], raw[Y][:], 0, 2)
-        deal(nc.vector.tensor_copy, grouped[Y][:], raw[Y][:], 2, 4)
+        deal(nc.scalar.copy, grouped[E][:], raw[E][:, :, 0:WIDTH], 0, 4)
+        for u in range(PIECES):
+            nc.sync.dma_start(out=raw_last[u][:], in_=w4.rearrange("(p j) c -> p j c", j=PACK)[:, :, CUTS[u] : CUTS[u + 1]])
+        deal(nc.scalar.copy, grouped[Y][:], raw[Y][:, :, 0:WIDTH], 0, 2)
+        deal(nc.vector.tensor_copy, grouped[Y][:], raw[Y][:, :, 0:WIDTH], 2, 4)
         quantize_weight(E)
         quantize_weight(Y)
-        deal(nc.scalar.copy, grouped[X][:], raw[X][:], 0, 2)
-        deal(nc.vector.tensor_copy, grouped[X][:], raw[X][:], 2, 4)
+        deal(nc.scalar.copy, grouped[X][:], raw[X][:, :, 0:WIDTH], 0, 2)
+        deal(nc.vector.tensor_copy, grouped[X][:], raw[X][:, :, 0:WIDTH], 2, 4)
         gather_words(Y)
         quantize_weight(X)
         gather_words(X)
@@ -171,24 +179,19 @@ def tile_picked_zlayout_gelu_po_kernel(
                 )
 
         h_bf = sb("h_bf", [P, CHUNKS, CHUNK, PACK], BF16)
-        h_codes = [sb("h_codes_0", [P, HALF], U32), at("h_codes_1", [P, HALF], U32, 16 * cuts[2])]
+        h_codes = [sb("h_codes_0", [P, HALF], U32), at("h_codes_1", [P, HALF], U32, 16 * CUTS[PIECES - 1])]
         h_scales = [sb("h_scales_%d" % h, [P, HALF], U8) for h in range(2)]
 
-        for c in range(CHUNKS):
-            first_layer_passes(E, c)
-        deal_last(0, nc.scalar.copy)
-        for c in range(CHUNKS):
-            for i in order(c)[1:]:
-                first_layer_passes(i, c)
+        def gelu(c):
             nc.scalar.activation(h_bf[:, c], hidden[c][:].rearrange("p t n -> p n t"), GELU)
 
         def quantize_hidden(c):
             cols = slice((c % 2) * CHUNK, (c % 2 + 1) * CHUNK)
             quantize(h_codes[c // 2][:, cols], h_scales[c // 2][:, cols], h_bf[:, c].rearrange("p n t -> p (n t)"))
 
-        def quantize_last(t):
-            slot = slice(t * P, (t + 1) * P)
-            quantize(w_codes[LAST][:, slot], w_scales[LAST][:, slot], last_grouped[:, t].rearrange("p m j -> p (m j)"))
+        def quantize_last(t, m0, m1):
+            slot = slice(t * P + m0, t * P + m1)
+            quantize(w_codes[LAST][:, slot], w_scales[LAST][:, slot], last_grouped[:, t, m0:m1, :].rearrange("p m j -> p (m j)"))
 
         out_all = sb("out_all", [P, PACK, TOKENS], F32)
         out_f32 = [out_all[:, :, h * HALF : (h + 1) * HALF] for h in range(2)]
@@ -232,12 +235,19 @@ def tile_picked_zlayout_gelu_po_kernel(
             cols = slice(c * CHUNK, (c + 1) * CHUNK)
             quantize(out_codes[:, cols], out_scales[:, cols], out_bf[c][:].rearrange("p n t -> p (n t)"))
 
+        for c in range(CHUNKS):
+            first_layer_passes(E, c)
+        deal_last(0, nc.scalar.copy)
+        for c in range(CHUNKS):
+            for i in order(c)[1:]:
+                first_layer_passes(i, c)
+            gelu(c)
         deal_last(1, nc.vector.tensor_copy)
         quantize_hidden(0)
         deal_last(2, nc.vector.tensor_copy)
         quantize_hidden(1)
         for t in range(PACK):
-            quantize_last(t)
+            quantize_last(t, 0, P)
             second_pass(single[t][:], 0, t)
         quantize_hidden(2)
         quantize_hidden(3)

@@ -50,16 +50,16 @@ def tile_picked_zlayout_gelu_po_kernel(
 
         lists = [sb("list_" + n, [P, TOKENS // 16], U16) for n in names]
         table_scales = [
-            at("scales_x", [P, columns[X]], U8, 8 * KB),
-            at("scales_e", [P, columns[E]], U8, 16 * KB),
-            at("scales_y", [P, columns[Y]], U8, 17 * KB),
+            at("scales_x", [P, columns[X]], U8, 10 * KB),
+            at("scales_e", [P, columns[E]], U8, 12 * KB),
+            at("scales_y", [P, columns[Y]], U8, 13 * KB),
         ]
         table_words = [
-            at("words_x", [P, columns[X]], I32, 20 * KB),
-            at("words_e", [P, columns[E]], I32, 20 * KB),
-            at("words_y", [P, columns[Y]], I32, 16 * KB),
+            at("words_x", [P, columns[X]], I32, 14 * KB),
+            at("words_e", [P, columns[E]], I32, 14 * KB),
+            at("words_y", [P, columns[Y]], I32, 10 * KB),
         ]
-        raw = [at("raw_x", [P, PACK, WIDTH], F32, 8 * KB), at("raw_e", [P, PACK, WIDTH], F32, 0), sb("raw_y", [P, PACK, WIDTH], F32)]
+        raw = [sb("raw_x", [P, PACK, WIDTH], F32), at("raw_e", [P, PACK, WIDTH], F32, 0), sb("raw_y", [P, PACK, WIDTH], F32)]
         raw_last = [at("raw_last_%d" % u, [P, PACK, CUTS[u + 1] - CUTS[u]], F32, 16 * CUTS[u]) for u in range(PIECES)]
         place = {X: 0, E: 0, Y: TOKENS}
         first_row = {X: 112, E: 48, Y: 48}
@@ -68,7 +68,7 @@ def tile_picked_zlayout_gelu_po_kernel(
         planes = {X: sb("planes_x", [P, TOKENS], U8)}
         picked_rows[E] = picked_rows[Y] = sb("picked_rows_ey", [P, 2 * TOKENS], U8)
         planes[E] = planes[Y] = sb("planes_ey", [P, 2 * TOKENS], U8)
-        moves = (X, E)
+        moves = ((X, nc.gpsimd), (E, nc.sync))
         warm_in = sb("warm_in", [P, 8], F32)
         warm_out = sb("warm_out", [P, 8], F32)
 
@@ -77,7 +77,7 @@ def tile_picked_zlayout_gelu_po_kernel(
             nc.vector.memset(table_scales[i][0 : first_row[i], :].bitcast(I32), 0)
             if first_row[i] + 16 < P:
                 nc.vector.memset(table_scales[i][first_row[i] + 16 : P, :].bitcast(I32), 0)
-        for i in moves:
+        for i, queue in moves:
             nc.vector.memset(planes[i][:].bitcast(I32), 0)
 
         def load_weight(i):
@@ -92,22 +92,17 @@ def tile_picked_zlayout_gelu_po_kernel(
         for i in (X, Y, E):
             nc.scalar.dma_start(out=table_scales[i][first_row[i] : first_row[i] + 16, :].bitcast(I32), in_=scales_in[i][0].bitcast(I32))
         nc.scalar.activation(warm_out[:], warm_in[:], GELU)
-        for i in (E, Y):
+        for i in (E, Y, X):
             load_weight(i)
 
         for i in (X, Y, E):
             nc.vector.tensor_copy(picked_rows[i][:, place[i] : place[i] + TOKENS], table_scales[i][:].indirect(lists[i][:]))
-
-        def move_scale_rows(i):
+        for i, queue in moves:
             for r in range(4):
-                nc.sync.dma_start(
+                queue.dma_start(
                     out=planes[i][plane_row[i] + r : P : 32, :].bitcast(I32),
                     in_=picked_rows[i][first_row[i] + r : first_row[i] + 16 : 4, :].bitcast(I32),
                 )
-
-        move_scale_rows(X)
-        load_weight(X)
-        move_scale_rows(E)
         load_words(Y)
 
         picked = [
@@ -202,7 +197,6 @@ def tile_picked_zlayout_gelu_po_kernel(
         out_words = out_1[0].rearrange("p n t -> p (n t)").bitcast(I32)
 
         single = [psum.tile([P, HALF], F32, name="single_%d" % t, offset=(4 + t) * BANK) for t in range(PACK)]
-        pair = [psum.tile([P, 2, HALF], F32, name="pair_%d" % u, offset=u * BANK) for u in range(2)]
 
         def second_pass(dst, h, t):
             slot = slice(t * P, (t + 1) * P)
@@ -251,8 +245,9 @@ def tile_picked_zlayout_gelu_po_kernel(
             second_pass(single[t][:], 0, t)
         quantize_hidden(2)
         quantize_hidden(3)
+        second = [psum.tile([P, HALF], F32, name="second_%d" % t, offset=t * BANK) for t in range(PACK)]
         for t in range(PACK):
-            second_pass(pair[t // 2][:, t % 2, :], 1, t)
+            second_pass(second[t][:], 1, t)
         for t in range(PACK):
             copy = nc.vector.tensor_copy if t == 2 else nc.scalar.copy
             copy(out=out_f32[0][:, t, :], in_=single[t][:])
@@ -260,9 +255,10 @@ def tile_picked_zlayout_gelu_po_kernel(
                 store_rows(0, 0, 1)
             if t == 2:
                 store_rows(0, 1, 3)
-        nc.scalar.copy(out=out_f32[1][:, 0:2, :], in_=pair[0][:])
-        store_rows(1, 0, 2)
-        nc.scalar.copy(out=out_f32[1][:, 2:4, :], in_=pair[1][:])
+        for t in range(PACK):
+            nc.scalar.copy(out=out_f32[1][:, t, :], in_=second[t][:])
+            if t == 1:
+                store_rows(1, 0, 2)
         rest = slice(2 * TOKENS + HALF, PACK * TOKENS)
         nc.sync.dma_start(out=out_rows.rearrange("p t n -> p (t n)")[:, rest], in_=out_all[:].rearrange("p t n -> p (t n)")[:, rest])
         round_out(0, nc.vector.tensor_copy)

@@ -59,7 +59,7 @@ def tile_picked_zlayout_gelu_po_kernel(
             at("words_e", [P, columns[E]], I32, 14 * KB),
             at("words_y", [P, columns[Y]], I32, 10 * KB),
         ]
-        raw = [sb("raw_x", [P, PACK, WIDTH], F32), at("raw_e", [P, PACK, WIDTH], F32, 0), sb("raw_y", [P, PACK, WIDTH], F32)]
+        raw = [sb("raw_x", [P, PACK, WIDTH], F32), sb("raw_e", [P, PACK, WIDTH], F32), at("raw_y", [P, PACK, WIDTH], F32, 0)]
         raw_last = [at("raw_last_%d" % u, [P, PACK, CUTS[u + 1] - CUTS[u]], F32, 16 * CUTS[u]) for u in range(PIECES)]
         place = {X: 0, E: 0, Y: TOKENS}
         first_row = {X: 112, E: 48, Y: 48}

from contextlib import ExitStack

import concourse.mybir as mybir

F32 = mybir.dt.float32
BF16 = mybir.dt.bfloat16
I32 = mybir.dt.int32
U32 = mybir.dt.uint32
U16 = mybir.dt.uint16
U8 = mybir.dt.uint8
FP8X4 = mybir.dt.float8_e4m3fn_x4
GELU = mybir.ActivationFunctionType.Gelu_apprx_tanh

P = 128
PACK = 4
WIDTH = 512
TOKENS = 512
CHUNK = 128
CHUNKS = TOKENS // CHUNK
HALF = TOKENS // 2
KB = 1024
BANK = 2048
FLOPS = 4 * 2 * 512 * 512 * 512
X, E, Y, LAST = 0, 1, 2, 3
CUTS = (0, 128, 384, 512)
PIECES = len(CUTS) - 1


def tile_picked_zlayout_gelu_po_kernel(
    tc, x_words, x_scales, e_words, e_scales, y_words, y_scales, w1, w2, w3, w4, offs, tok, row, out_0, out_1, out_2
):
    nc = tc.nc
    with ExitStack() as ctx:
        keep = ctx.enter_context(tc.tile_pool(name="keep", bufs=1))
        shared = ctx.enter_context(tc.tile_pool(name="shared", bufs=1))
        psum = ctx.enter_context(tc.psum_pool(name="psum", bufs=1))

        def sb(name, shape, dtype):
            return keep.tile(shape, dtype, name=name, align_bytes=64)

        def at(name, shape, dtype, offset):
            return shared.tile(shape, dtype, name=name, offset=offset, align_bytes=64)

        names = ("x", "e", "y")
        words_in = (x_words, e_words, y_words)
        scales_in = (x_scales, e_scales, y_scales)
        lists_in = (offs, tok, row)
        weights_in = (w1, w2, w3)
        columns = [w.shape[2] for w in words_in]

        lists = [sb("list_" + n, [P, TOKENS // 16], U16) for n in names]
        table_scales = [
            at("scales_x", [P, columns[X]], U8, 10 * KB),
            at("scales_e", [P, columns[E]], U8, 12 * KB),
            at("scales_y", [P, columns[Y]], U8, 13 * KB),
        ]
        table_words = [
            at("words_x", [P, columns[X]], I32, 14 * KB),
            at("words_e", [P, columns[E]], I32, 14 * KB),
            at("words_y", [P, columns[Y]], I32, 10 * KB),
        ]
        raw = [sb("raw_x", [P, PACK, WIDTH], F32), sb("raw_e", [P, PACK, WIDTH], F32), at("raw_y", [P, PACK, WIDTH], F32, 0)]
        raw_last = [at("raw_last_%d" % u, [P, PACK, CUTS[u + 1] - CUTS[u]], F32, 16 * CUTS[u]) for u in range(PIECES)]
        place = {X: 0, E: 0, Y: TOKENS}
        first_row = {X: 112, E: 48, Y: 48}
        plane_row = {X: 0, E: 4, Y: 4}
        picked_rows = {X: sb("picked_rows_x", [P, TOKENS], U8)}
        planes = {X: sb("planes_x", [P, TOKENS], U8)}
        picked_rows[E] = picked_rows[Y] = sb("picked_rows_ey", [P, 2 * TOKENS], U8)
        planes[E] = planes[Y] = sb("planes_ey", [P, 2 * TOKENS], U8)
        moves = ((X, nc.gpsimd), (E, nc.sync))
        warm_in = sb("warm_in", [P, 8], F32)
        warm_out = sb("warm_out", [P, 8], F32)

        nc.vector.memset(warm_in[:], 0.0)
        for i in (X, Y, E):
            nc.vector.memset(table_scales[i][0 : first_row[i], :].bitcast(I32), 0)
            if first_row[i] + 16 < P:
                nc.vector.memset(table_scales[i][first_row[i] + 16 : P, :].bitcast(I32), 0)
        for i, queue in moves:
            nc.vector.memset(planes[i][:].bitcast(I32), 0)

        def load_weight(i):
            nc.sync.dma_start(out=raw[i][:, :, 0:WIDTH], in_=weights_in[i].rearrange("(p j) c -> p j c", j=PACK))

        def load_words(i):
            nc.sync.dma_start(out=table_words[i][:], in_=words_in[i][0].rearrange("p n t -> p (n t)").bitcast(I32))

        load_words(E)
        for i in (X, Y, E):
            nc.sync.dma_start(lists[i][:], lists_in[i])
        for i in (X, Y, E):
            nc.scalar.dma_start(out=table_scales[i][first_row[i] : first_row[i] + 16, :].bitcast(I32), in_=scales_in[i][0].bitcast(I32))
        nc.scalar.activation(warm_out[:], warm_in[:], GELU)
        for i in (E, Y, X):
            load_weight(i)

        for i in (X, Y, E):
            nc.vector.tensor_copy(picked_rows[i][:, place[i] : place[i] + TOKENS], table_scales[i][:].indirect(lists[i][:]))
        for i, queue in moves:
            for r in range(4):
                queue.dma_start(
                    out=planes[i][plane_row[i] + r : P : 32, :].bitcast(I32),
                    in_=picked_rows[i][first_row[i] + r : first_row[i] + 16 : 4, :].bitcast(I32),
                )
        load_words(Y)

        picked = [
            [sb("picked_x_%d" % c, [P, CHUNK], U32) for c in range(CHUNKS)],
            [sb("picked_e", [P, TOKENS], U32)],
            [sb("picked_y_%d" % h, [P, HALF], U32) for h in range(2)],
        ]

        def gather_words(i):
            step = TOKENS // 16 // len(picked[i])
            for n, tile in enumerate(picked[i]):
                nc.vector.tensor_copy(tile[:], table_words[i][:].bitcast(U32).indirect(lists[i][:, n * step : (n + 1) * step]))

        gather_words(E)
        load_words(X)

        grouped = [sb("grouped_" + n, [P, PACK, P, PACK], BF16) for n in names]
        last_grouped = sb("last_grouped", [P, PACK, P, PACK], BF16)
        w_codes = [sb("w_codes_%d" % i, [P, WIDTH], U32) for i in range(4)]
        w_scales = [sb("w_scales_%d" % i, [P, WIDTH], U8) for i in range(4)]

        def deal(copy, dst, src, t0, t1):
            copy(
                out=dst[:, t0:t1].rearrange("p t m j -> p m j t"),
                in_=src.rearrange("p j (m t) -> p m j t", t=PACK)[:, :, :, t0:t1],
            )

        def deal_last(u, copy, c0=0, c1=None):
            c1 = CUTS[u + 1] - CUTS[u] if c1 is None else c1
            deal(copy, last_grouped[:, :, (CUTS[u] + c0) // PACK : (CUTS[u] + c1) // PACK, :], raw_last[u][:, :, c0:c1], 0, PACK)

        def quantize(codes, scales, values):
            nc.vector.quantize_mx(out=codes.bitcast(FP8X4), scales=scales, in_=values)

        def quantize_weight(i):
            quantize(w_codes[i][:], w_scales[i][:], grouped[i][:].rearrange("p t m j -> p (t m j)"))

        deal(nc.scalar.copy, grouped[E][:], raw[E][:, :, 0:WIDTH], 0, 4)
        for u in range(PIECES):
            nc.sync.dma_start(out=raw_last[u][:], in_=w4.rearrange("(p j) c -> p j c", j=PACK)[:, :, CUTS[u] : CUTS[u + 1]])
        deal(nc.scalar.copy, grouped[Y][:], raw[Y][:, :, 0:WIDTH], 0, 2)
        deal(nc.vector.tensor_copy, grouped[Y][:], raw[Y][:, :, 0:WIDTH], 2, 4)
        quantize_weight(E)
        quantize_weight(Y)
        deal(nc.scalar.copy, grouped[X][:], raw[X][:, :, 0:WIDTH], 0, 2)
        deal(nc.vector.tensor_copy, grouped[X][:], raw[X][:, :, 0:WIDTH], 2, 4)
        gather_words(Y)
        quantize_weight(X)
        gather_words(X)

        hidden = [psum.tile([P, PACK, CHUNK], F32, name="hidden_%d" % c, offset=c * BANK) for c in range(CHUNKS)]

        def order(c):
            return (E, Y, X) if c < 2 else (E, X, Y)

        def first_layer_passes(i, c):
            per_tile = CHUNKS // len(picked[i])
            codes = picked[i][c // per_tile][:, (c % per_tile) * CHUNK : (c % per_tile + 1) * CHUNK]
            for t in range(PACK):
                slot = slice(t * P, (t + 1) * P)
                nc.tensor.matmul_mx(
                    out=hidden[c][:, t, :],
                    lhsT=w_codes[i][:, slot].bitcast(FP8X4),
                    lhsT_scale=w_scales[i][:, slot],
                    rhs=codes.bitcast(FP8X4),
                    rhs_scale=planes[i][plane_row[i] : P, place[i] + c * CHUNK : place[i] + (c + 1) * CHUNK],
                    start=(i == E and t == 0),
                    stop=(i == order(c)[2] and t == PACK - 1),
                )

        h_bf = sb("h_bf", [P, CHUNKS, CHUNK, PACK], BF16)
        h_codes = [sb("h_codes_0", [P, HALF], U32), at("h_codes_1", [P, HALF], U32, 16 * CUTS[PIECES - 1])]
        h_scales = [sb("h_scales_%d" % h, [P, HALF], U8) for h in range(2)]

        def gelu(c):
            nc.scalar.activation(h_bf[:, c], hidden[c][:].rearrange("p t n -> p n t"), GELU)

        def quantize_hidden(c):
            cols = slice((c % 2) * CHUNK, (c % 2 + 1) * CHUNK)
            quantize(h_codes[c // 2][:, cols], h_scales[c // 2][:, cols], h_bf[:, c].rearrange("p n t -> p (n t)"))

        def quantize_last(t, m0, m1):
            slot = slice(t * P + m0, t * P + m1)
            quantize(w_codes[LAST][:, slot], w_scales[LAST][:, slot], last_grouped[:, t, m0:m1, :].rearrange("p m j -> p (m j)"))

        out_all = sb("out_all", [P, PACK, TOKENS], F32)
        out_f32 = [out_all[:, :, h * HALF : (h + 1) * HALF] for h in range(2)]
        out_bf = [sb("out_bf_%d" % c, [P, CHUNK, PACK], BF16) for c in range(CHUNKS)]
        out_codes = sb("out_codes", [P, TOKENS], U32)
        out_scales = sb("out_scales", [P, TOKENS], U8)
        out_rows = out_0.rearrange("(p t) n -> p t n", t=PACK)
        out_words = out_1[0].rearrange("p n t -> p (n t)").bitcast(I32)

        single = [psum.tile([P, HALF], F32, name="single_%d" % t, offset=(4 + t) * BANK) for t in range(PACK)]

        def second_pass(dst, h, t):
            slot = slice(t * P, (t + 1) * P)
            nc.tensor.matmul_mx(
                out=dst,
                lhsT=w_codes[LAST][:, slot].bitcast(FP8X4),
                lhsT_scale=w_scales[LAST][:, slot],
                rhs=h_codes[h][:].bitcast(FP8X4),
                rhs_scale=h_scales[h][:],
                start=True,
                stop=True,
            )

        def tokens(h):
            return slice(h * HALF, (h + 1) * HALF)

        def store_rows(h, t0, t1):
            nc.sync.dma_start(out=out_rows[:, t0:t1, tokens(h)], in_=out_f32[h][:, t0:t1, :])

        def store_codes(h):
            nc.sync.dma_start(out=out_words[:, tokens(h)], in_=out_codes[:, tokens(h)].bitcast(I32))

        def round_out(c, copy):
            copy(
                out=out_bf[c][:].rearrange("p (a b) t -> p a t b", b=4),
                in_=out_f32[c // 2][:, :, (c % 2) * CHUNK : (c % 2 + 1) * CHUNK].rearrange("p t (a b) -> p a t b", b=4),
            )

        def quantize_out(c):
            cols = slice(c * CHUNK, (c + 1) * CHUNK)
            quantize(out_codes[:, cols], out_scales[:, cols], out_bf[c][:].rearrange("p n t -> p (n t)"))

        for c in range(CHUNKS):
            first_layer_passes(E, c)
        deal_last(0, nc.scalar.copy)
        for c in range(CHUNKS):
            for i in order(c)[1:]:
                first_layer_passes(i, c)
            gelu(c)
        deal_last(1, nc.vector.tensor_copy)
        quantize_hidden(0)
        deal_last(2, nc.vector.tensor_copy)
        quantize_hidden(1)
        for t in range(PACK):
            quantize_last(t, 0, P)
            second_pass(single[t][:], 0, t)
        quantize_hidden(2)
        quantize_hidden(3)
        second = [psum.tile([P, HALF], F32, name="second_%d" % t, offset=t * BANK) for t in range(PACK)]
        for t in range(PACK):
            second_pass(second[t][:], 1, t)
        for t in range(PACK):
            copy = nc.vector.tensor_copy if t == 2 else nc.scalar.copy
            copy(out=out_f32[0][:, t, :], in_=single[t][:])
            if t == 0:
                store_rows(0, 0, 1)
            if t == 2:
                store_rows(0, 1, 3)
        for t in range(PACK):
            nc.scalar.copy(out=out_f32[1][:, t, :], in_=second[t][:])
            if t == 1:
                store_rows(1, 0, 2)
        rest = slice(2 * TOKENS + HALF, PACK * TOKENS)
        nc.sync.dma_start(out=out_rows.rearrange("p t n -> p (t n)")[:, rest], in_=out_all[:].rearrange("p t n -> p (t n)")[:, rest])
        round_out(0, nc.vector.tensor_copy)
        round_out(1, nc.vector.tensor_copy)
        quantize_out(0)
        quantize_out(1)
        store_codes(0)
        round_out(2, nc.vector.tensor_copy)
        round_out(3, nc.scalar.copy)
        quantize_out(2)
        quantize_out(3)
        store_codes(1)
        for q in range(4):
            queue = nc.scalar if q else nc.sync
            queue.dma_start(out=out_2[0, q:16:4, :].bitcast(I32), in_=out_scales[q:P:32, :].bitcast(I32))
